import numpy as np
import ml_dtypes


def mxq(x, axis, fmt="e4m3"):
    dtype, down = {"e4m3": (ml_dtypes.float8_e4m3fn, 7), "e5m2": (ml_dtypes.float8_e5m2, 14)}[fmt]
    v = np.moveaxis(np.asarray(x, np.float32).astype(ml_dtypes.bfloat16).astype(np.float64), axis, -1)
    blocks = v.reshape(v.shape[:-1] + (-1, 32))
    amax = np.abs(blocks).max(-1, keepdims=True)
    byte = np.maximum(np.where(amax > 0, np.frexp(amax)[1] - 1 + 127, 0) - down, 1)
    scale = np.exp2(byte - 127.0)
    codes = (blocks / scale).astype(np.float32).astype(dtype).astype(np.float64)
    return np.moveaxis((codes * scale).reshape(v.shape), -1, axis)


WIDE = False


def mx_kscale(k):
    if not WIDE:
        return np.ones(k)
    levels = np.array([10, -10, 5, -5, 0])
    if k % 512:
        return np.exp2(np.random.permutation(np.resize(levels, k // 32))).repeat(32)
    a = np.empty((k // 512, 16))
    for p in range(k // 512):
        a[p, :8] = np.random.permutation(np.resize(levels, 8))
        for g in range(8):
            far = levels[np.abs(levels - a[p, g]) >= 10]
            a[p, g + 8] = far[np.random.randint(len(far))]
    return np.exp2(a.ravel()).repeat(32)


BF16 = ml_dtypes.bfloat16


def bf(x):
    return np.asarray(x, np.float32).astype(BF16)


def f64(x):
    return np.asarray(x).astype(np.float64)


E2M1 = np.array([0.0, 0.5, 1.0, 1.5, 2.0, 3.0, 4.0, 6.0, -0.0, -0.5, -1.0, -1.5, -2.0, -3.0, -4.0, -6.0])


def pack_weight(w, fmt):
    k, n = w.shape
    w = f64(bf(w)).reshape(k // 32, 32, n)
    amax = np.abs(w).max(1)
    if fmt == "e4m3":
        byte = np.frexp(amax)[1] - 1 + 127 - 7
    else:
        mant, ex = np.frexp(amax / 6.0)
        byte = np.where(mant > 0.5, ex, ex - 1) + 127
    byte = np.clip(np.where(amax > 0, byte, 1), 1, 254)
    scaled = (w * np.exp2(127.0 - byte)[:, None, :]).reshape(k, n).astype(np.float32)
    by_word = np.ascontiguousarray(scaled.reshape(k // 512, 128, 4, n).transpose(0, 1, 3, 2))
    if fmt == "e4m3":
        words = by_word.astype(ml_dtypes.float8_e4m3fn).view(np.uint8)
    else:
        c = by_word.astype(ml_dtypes.float4_e2m1fn).view(np.uint8) & 0xF
        words = c[..., 0::2] | (c[..., 1::2] << 4)
    return np.ascontiguousarray(words), np.ascontiguousarray(byte.astype(np.uint8).reshape(k // 512, 16, n))


def unpack_weight(words, scales, fmt):
    g, p, n, _ = words.shape
    if fmt == "e4m3":
        vals = np.ascontiguousarray(words).view(ml_dtypes.float8_e4m3fn).astype(np.float64)
    else:
        nib = np.empty((g, p, n, 4), np.uint8)
        nib[..., 0::2] = words & 0xF
        nib[..., 1::2] = words >> 4
        vals = E2M1[nib]
    vals = vals * np.repeat(np.exp2(scales.astype(np.float64) - 127.0), 8, axis=1)[..., None]
    return vals.transpose(0, 1, 3, 2).reshape(g * 512, n)
def pack4(w):
    words, scales = pack_weight(w, "e2m1")
    return words.reshape(words.shape[0], 128, -1), scales


def unpack4(words, scales):
    return unpack_weight(words.reshape(words.shape[0], 128, -1, 2), scales, "e2m1")


B, E, D, S = 1024, 1024, 512, 2048


def draw0():
    s, u, t = mx_kscale(E), mx_kscale(D), mx_kscale(S)
    counts = np.random.randint(-3, 4, (E, S)).astype(np.float64)
    mass = np.random.uniform(0.5, 1.5, E)
    f_words, f_scales = pack4(counts / (2 * np.sqrt(E)) / s[:, None])
    a_words, a_scales = pack4(counts.T * mass / (2 * np.sqrt(S)) / t[:, None])
    return {"lam": bf(0.6 * np.random.standard_normal((B, E)) * s),
            "f_words": f_words, "f_scales": f_scales,
            "phi": bf(0.5 * np.random.standard_normal((B, D)) * u),
            "g": bf(np.random.standard_normal((D, S)) / np.sqrt(D) / u[:, None]),
            "m": bf(np.random.uniform(0.5, 1.5, S) * t),
            "a_words": a_words, "a_scales": a_scales,
            "feed": bf(np.random.standard_normal((B, E)))}


def core(lam, f_words, f_scales, phi, g, m, a_words, a_scales, feed):
    F = unpack4(f_words, f_scales)
    A = unpack4(a_words, a_scales)
    z = (mxq(f64(lam), 1, "e4m3") @ F) + (mxq(f64(phi), 1, "e4m3") @ mxq(f64(g), 0, "e4m3"))
    n = np.exp(z) * f64(m)
    return (mxq(n, 1, "e4m3") @ A) - f64(feed)


def e4m3fn_bytes(y):
    return np.clip(np.asarray(y, np.float64), -448.0, 448.0).astype(np.float32).astype(ml_dtypes.float8_e4m3fn).view(np.uint8)


def e4m3fn_values(b):
    return np.asarray(b, np.uint8).view(ml_dtypes.float8_e4m3fn).astype(np.float64)


def setup_inputs():
    d = draw0()
    x0 = np.asarray(d['lam']).astype(np.float64)
    s = (np.max(np.abs(x0), axis=(0,), keepdims=True) / 448.0).astype(np.float32)
    out = {}
    for k, v in d.items():
        if k == 'lam':
            out['lam_bytes'] = e4m3fn_bytes(x0 / s.astype(np.float64))
            out['lam_scale'] = s
        else:
            out[k] = v
    return out


def reference(lam_bytes, lam_scale, f_words, f_scales, phi, g, m, a_words, a_scales, feed):
    return core(e4m3fn_values(lam_bytes) * lam_scale.astype(np.float64), f_words, f_scales, phi, g, m, a_words, a_scales, feed)

@@ -1,0 +1,439 @@
+from contextlib import ExitStack
+
+import concourse.mybir as mybir
+from concourse.masks import make_identity
+
+B, E, D, S = 1024, 1024, 512, 2048
+FLOPS = 2 * B * S * (E + D) + 2 * B * S * E
+
+F32 = mybir.dt.float32
+BF16 = mybir.dt.bfloat16
+U32 = mybir.dt.uint32
+I32 = mybir.dt.int32
+U8 = mybir.dt.uint8
+FP8 = mybir.dt.float8_e4m3fn
+FP8X4 = mybir.dt.float8_e4m3fn_x4
+FP4X4 = mybir.dt.float4_e2m1fn_x4
+ALU = mybir.AluOpType
+ACT = mybir.ActivationFunctionType
+
+P = 128
+HALF = 512
+ROWS = 4
+UNITS = S // 512
+LG = E // 512
+
+
+def tile_equilibrium_mass_balance_s3_kernel(
+    tc, lam_bytes, lam_scale, f_words, f_scales, phi, g, m, a_words, a_scales, feed, out
+):
+    nc = tc.nc
+    with ExitStack() as ctx:
+        keep = ctx.enter_context(tc.tile_pool(name="keep", bufs=1))
+        work = ctx.enter_context(tc.tile_pool(name="work", bufs=2))
+        psum = ctx.enter_context(tc.psum_pool(name="psum", bufs=1))
+
+        lam_v = lam_bytes.rearrange("(h p c) k -> h p c k", h=2, c=ROWS)
+        phi_v = phi.rearrange("(h p c) k -> h p c k", h=2, c=ROWS)
+        feed_v = feed.rearrange("(h p c) e -> h p c e", h=2, c=ROWS)
+        out_v = out.rearrange("(h p c) e -> h p c e", h=2, c=ROWS)
+        g_v = g.rearrange("(p j) s -> p j s", j=4)
+        f_v = f_words.rearrange("k p b -> p k b")
+        a_v = a_words.rearrange("k p b -> p k b")
+
+        f_sc_raw = keep.tile([P, LG, S], U8, name="f_sc_raw", align_bytes=64)
+        nc.vector.memset(f_sc_raw[:].bitcast(I32), 0)
+        ident = keep.tile([P, P], F32, name="ident")
+        make_identity(nc, ident[:])
+        a_sc = keep.tile([P, UNITS, E], U8, name="a_sc", align_bytes=64)
+        nc.gpsimd.memset(a_sc[:].bitcast(I32), 0)
+        warm = keep.tile([P, 1], F32, name="warm")
+        nc.vector.memset(warm[:], 0.0)
+        nc.scalar.activation(warm[:], warm[:], ACT.Exp)
+
+        lam_sb, phi_sb, feed_sb = [], [], []
+        for h in range(2):
+            t8 = keep.tile([P, ROWS, E], U8, name="lam_sb%d" % h)
+            tb = keep.tile([P, ROWS, D], BF16, name="phi_sb%d" % h)
+            tf = keep.tile([P, ROWS, E], BF16, name="feed_sb%d" % h)
+            lam_sb.append(t8)
+            phi_sb.append(tb)
+            feed_sb.append(tf)
+
+        def load_rows(dst, src, h, cs):
+            nc.sync.dma_start(out=dst[h][:, cs, :], in_=src[h][:, cs, :])
+
+        g_sb, f_sb = {}, {}
+
+        def load_g(u0, n):
+            t = keep.tile([P, 4, 512 * n], BF16, name="g_sb%d" % u0)
+            nc.sync.dma_start(out=t[:], in_=g_v[:, :, 512 * u0 : 512 * (u0 + n)])
+            for i in range(n):
+                g_sb[u0 + i] = t[:, :, 512 * i : 512 * (i + 1)]
+
+        def load_f(u0, n):
+            t = keep.tile([P, LG, 1024 * n], U8, name="f_sb%d" % u0)
+            nc.sync.dma_start(out=t[:], in_=f_v[:, :, 1024 * u0 : 1024 * (u0 + n)])
+            for i in range(n):
+                f_sb[u0 + i] = t[:, :, 1024 * i : 1024 * (i + 1)]
+
+        a_sb = keep.tile([P, UNITS, 2 * E], U8, name="a_sb", align_bytes=64)
+
+        def load_scales(dst, src):
+            rows = src.bitcast(I32).rearrange("k (q r) n -> r q k n", r=4)
+            words = dst[:].bitcast(I32)
+            for r in range(4):
+                nc.sync.dma_start(out=words[r:P:32], in_=rows[r])
+
+        l_sc = keep.tile([P, LG, 4], F32, name="l_sc")
+        m_sb = keep.tile([P, UNITS, 4], BF16, name="m_sb")
+        m_f = keep.tile([P, UNITS * 4], F32, name="m_f")
+
+        load_rows(lam_sb, lam_v, 0, slice(0, 2))
+        load_f(0, 1)
+        load_scales(f_sc_raw, f_scales)
+        nc.sync.dma_start(out=l_sc[:], in_=lam_scale.rearrange("o (k p t) -> p (o k) t", p=P, t=4))
+        load_rows(lam_sb, lam_v, 0, slice(2, 4))
+        load_rows(phi_sb, phi_v, 0, slice(0, 4))
+        load_g(0, 1)
+        load_f(1, 1)
+        load_g(1, 1)
+        load_rows(phi_sb, phi_v, 1, slice(0, 4))
+        nc.sync.dma_start(out=m_sb[:], in_=m.rearrange("(u p t) -> p u t", p=P, t=4))
+        nc.gpsimd.tensor_copy(out=m_f[:], in_=m_sb[:].rearrange("p u t -> p (u t)"))
+        load_f(2, 2)
+        load_g(2, 2)
+        load_rows(lam_sb, lam_v, 1, slice(0, 4))
+        load_scales(a_sc, a_scales)
+        nc.sync.dma_start(out=a_sb[:], in_=a_v)
+        for h in range(2):
+            load_rows(feed_sb, feed_v, h, slice(0, 4))
+
+        phi_q, phi_s, lam_q, lam_s, phi_t, lam_t, tps, casts = {}, {}, {}, {}, {}, {}, {}, {}
+
+        def begin(h):
+            phi_t[h] = work.tile([P, HALF, 4], BF16, name="phi_t", tag="phi_t", bufs=2, align_bytes=64)
+            phi_q[h] = keep.tile([P, HALF], U32, name="phi_q%d" % h, align_bytes=64)
+            phi_s[h] = keep.tile([P, HALF], U8, name="phi_s%d" % h, align_bytes=64)
+            lam_t[h] = work.tile([P, LG, HALF, 4], BF16, name="lam_t", tag="lam_t", bufs=1, align_bytes=64)
+            lam_q[h] = keep.tile([P, LG, HALF], U32, name="lam_q%d" % h, align_bytes=64)
+            lam_s[h] = keep.tile([P, LG, HALF], U8, name="lam_s%d" % h, align_bytes=64)
+
+        def phi_turn(h, pair):
+            tps[h, "p", pair] = psum.tile([P, 512], F32, name="tp", tag="acc", bufs=4)
+            for i in range(2):
+                words = phi_sb[h][:, 2 * pair + i, :].bitcast(F32)
+                for u in range(2):
+                    k = 128 * (2 * i + u)
+                    nc.tensor.transpose(tps[h, "p", pair][:, k : k + 128], words[:, u::2], ident[:])
+
+        def phi_copy(h, pair):
+            dst = phi_t[h][:].rearrange("p r t -> p (r t)").bitcast(F32)
+            dst = dst.rearrange("p (c r u) -> p c r u", c=4, u=2)
+            nc.scalar.copy(
+                dst[:, 2 * pair : 2 * pair + 2], tps[h, "p", pair][:].rearrange("p (c u r) -> p c r u", c=2, u=2)
+            )
+
+        def phi_quant(h):
+            nc.vector.quantize_mx(
+                out=phi_q[h][:].bitcast(FP8X4), scales=phi_s[h][:], in_=phi_t[h][:].rearrange("p r t -> p (r t)")
+            )
+
+        def lam_cast(h, c):
+            casts[h, c] = work.tile([P, E], BF16, name="cast", tag="cast", bufs=3)
+            nc.scalar.copy(casts[h, c][:], lam_sb[h][:, c, :].bitcast(FP8))
+
+        def lam_turn(h, c):
+            words = casts[h, c][:].bitcast(F32)
+            tps[h, c] = psum.tile([P, 512], F32, name="tp", tag="acc", bufs=4)
+            for k in range(LG):
+                for u in range(2):
+                    b = 128 * (2 * k + u)
+                    nc.tensor.transpose(
+                        tps[h, c][:, b : b + 128], words[:, 256 * k + u : 256 * (k + 1) : 2], ident[:]
+                    )
+
+        def lam_mult(h, c):
+            for k in range(LG):
+                vals = tps[h, c][:, 256 * k : 256 * (k + 1)].bitcast(BF16)
+                nc.vector.tensor_tensor(
+                    out=lam_t[h][:, k, 128 * c : 128 * (c + 1), :].rearrange("p r (u e) -> p r u e", e=2),
+                    in0=vals.rearrange("p (u r e) -> p r u e", u=2, e=2),
+                    in1=l_sc[:, k, :].rearrange("p (u e) -> p u e", e=2).unsqueeze(1).to_broadcast([P, P, 2, 2]),
+                    op=ALU.mult,
+                )
+
+        def lam_quant(h, k):
+            nc.vector.quantize_mx(
+                out=lam_q[h][:, k, :].bitcast(FP8X4),
+                scales=lam_s[h][:, k, :],
+                in_=lam_t[h][:, k].rearrange("p r t -> p (r t)"),
+            )
+
+        g_q, g_s, f_p, f_sp, g_i = {}, {}, {}, {}, {}
+
+        def g_lay(u, i, copy):
+            if u not in g_i:
+                g_i[u] = work.tile([P, 512, 4], BF16, name="gi", tag="gi", bufs=2, align_bytes=64)
+            ms = slice(64 * i, 64 * i + 64)
+            copy(
+                g_i[u][:].rearrange("p (t m) j -> p m t j", t=4)[:, ms],
+                g_sb[u].rearrange("p j (m t) -> p m t j", t=4)[:, ms],
+            )
+
+        def g_quant(u):
+            g_q[u] = keep.tile([P, 512], U32, name="g_q%d" % u, align_bytes=64)
+            g_s[u] = keep.tile([P, 512], U8, name="g_s%d" % u, align_bytes=64)
+            nc.vector.quantize_mx(
+                out=g_q[u][:].bitcast(FP8X4), scales=g_s[u][:], in_=g_i[u][:].rearrange("p s j -> p (s j)")
+            )
+
+        def f_move(u):
+            f_p[u] = keep.tile([P, LG, 1024], U8, name="f_p%d" % u, align_bytes=64)
+            for k in range(LG):
+                nc.vector.tensor_copy(
+                    out=f_p[u][:, k, :].rearrange("p (t m b) -> p t m b", t=4, b=2),
+                    in_=f_sb[u][:, k, :].rearrange("p (m t b) -> p t m b", t=4, b=2),
+                )
+
+        def f_scale(u):
+            f_sp[u] = keep.tile([P, LG, 512], U8, name="f_sp%d" % u, align_bytes=64)
+            nc.vector.tensor_copy(
+                out=f_sp[u][:].rearrange("p k (t m) -> p k t m", t=4),
+                in_=f_sc_raw[:, :, 512 * u : 512 * (u + 1)].rearrange("p k (m t) -> p k t m", t=4),
+            )
+
+        e_sb, flat, nb, n_q, n_s = {}, {}, {}, {}, {}
+
+        z_ps = {}
+
+        def z_lam(h, u, t, k):
+            if k == 0:
+                z_ps[h, u, t] = psum.tile([P, HALF], F32, name="zp", tag="z", bufs=4)
+            nc.tensor.matmul_mx(
+                out=z_ps[h, u, t][:],
+                lhsT=f_p[u][:, k, 256 * t : 256 * (t + 1)].bitcast(FP4X4),
+                lhsT_scale=f_sp[u][:, k, 128 * t : 128 * (t + 1)],
+                rhs=lam_q[h][:, k, :].bitcast(FP8X4),
+                rhs_scale=lam_s[h][:, k, :],
+                start=(k == 0), stop=False,
+            )
+
+        def z_phi(h, u, t):
+            cols = slice(128 * t, 128 * (t + 1))
+            nc.tensor.matmul_mx(
+                out=z_ps[h, u, t][:], lhsT=g_q[u][:, cols].bitcast(FP8X4), lhsT_scale=g_s[u][:, cols],
+                rhs=phi_q[h][:].bitcast(FP8X4), rhs_scale=phi_s[h][:], start=False, stop=True,
+            )
+
+        def exp(h, u, t):
+            if t == 0:
+                e_sb[h, u] = work.tile([P, 4, HALF], F32, name="e_sb", tag="e_sb", bufs=5)
+            nc.scalar.activation(e_sb[h, u][:, t, :], z_ps[h, u, t][:], ACT.Exp)
+
+        def z_exp(h, u, t):
+            for k in range(LG):
+                z_lam(h, u, t, k)
+            z_phi(h, u, t)
+            exp(h, u, t)
+
+        def n_begin(h, u):
+            nb[h, u] = work.tile([P, HALF, 4], BF16, name="nb", tag="nb", bufs=2, align_bytes=64)
+            n_q[h, u] = keep.tile([P, HALF], U32, name="n_q%d%d" % (h, u), align_bytes=64)
+            n_s[h, u] = keep.tile([P, HALF], U8, name="n_s%d%d" % (h, u), align_bytes=64)
+
+        def n_scale(h, u, t):
+            if t == 0:
+                flat[h, u] = work.tile([P, 4, HALF], BF16, name="flat", tag="flat", bufs=2)
+            nc.scalar.activation(
+                flat[h, u][:, t, :], e_sb[h, u][:, t, :], ACT.Copy, scale=m_f[:, 4 * u + t : 4 * u + t + 1]
+            )
+
+        def n_lay(h, u, cols):
+            nc.vector.tensor_copy(
+                out=nb[h, u][:, cols, :].rearrange("p (r i) t -> p r t i", i=4),
+                in_=flat[h, u][:, :, cols].rearrange("p t (r i) -> p r t i", i=4),
+            )
+
+        def n_mult(h, u, cols):
+            nc.vector.tensor_tensor(
+                out=nb[h, u][:, cols, :].rearrange("p (r i) t -> p r t i", i=4),
+                in0=e_sb[h, u][:, :, cols].rearrange("p t (r i) -> p r t i", i=4),
+                in1=m_sb[:, u, :].unsqueeze(1).unsqueeze(3).to_broadcast([P, (cols.stop - cols.start) // 4, 4, 4]),
+                op=ALU.mult,
+            )
+
+        def n_quant(h, u, cols):
+            nc.vector.quantize_mx(
+                out=n_q[h, u][:, cols].bitcast(FP8X4),
+                scales=n_s[h, u][:, cols],
+                in_=nb[h, u][:, cols, :].rearrange("p r t -> p (r t)"),
+            )
+
+        acc = {}
+
+        def balance(h, u, e, c):
+            if u == 0:
+                tag = ("acc", 4) if e == 0 else ("z", 4)
+                acc[h, c, e] = psum.tile([P, 512], F32, name="ac", tag=tag[0], bufs=tag[1])
+            cols = slice(128 * c, 128 * (c + 1))
+            nc.tensor.matmul_mx(
+                out=acc[h, c, e][:],
+                lhsT=n_q[h, u][:, cols].bitcast(FP8X4), lhsT_scale=n_s[h, u][:, cols],
+                rhs=a_sb[:, u, 1024 * e : 1024 * (e + 1)].bitcast(FP4X4),
+                rhs_scale=a_sc[:, u, 512 * e : 512 * (e + 1)],
+                start=(u == 0), stop=(u == UNITS - 1),
+            )
+
+        def finish(h, e, c, parts=1):
+            w = 512 // parts
+            for i in range(parts):
+                cols = slice(512 * e + w * i, 512 * e + w * (i + 1))
+                o = work.tile([P, w], F32, name="o", tag="o", bufs=8)
+                nc.vector.tensor_tensor(
+                    out=o[:], in0=acc[h, c, e][:, w * i : w * (i + 1)], in1=feed_sb[h][:, c, cols], op=ALU.subtract
+                )
+                nc.sync.dma_start(out=out_v[h][:, c, cols], in_=o[:])
+
+        def warm_up(n):
+            wp = psum.tile([P, 512], F32, name="wp", tag="acc", bufs=4)
+            for i in range(n):
+                nc.tensor.matmul(
+                    wp[:], lhsT=phi_sb[0][:, 0, 0:P], rhs=phi_sb[0][:, 0, :], start=True, stop=True
+                )
+
+        ROW4 = range(4)
+        halves = [slice(0, 256), slice(256, 512)]
+        quarters = [slice(128 * c, 128 * c + 128) for c in ROW4]
+        vc, sc = nc.vector.tensor_copy, nc.scalar.copy
+
+        def n_vector(h, u):
+            n_begin(h, u)
+            for cols in halves:
+                n_mult(h, u, cols)
+            for cols in halves:
+                n_quant(h, u, cols)
+
+        def n_layq(h, u):
+            n_begin(h, u)
+            for cols in halves:
+                n_lay(h, u, cols)
+            for cols in halves:
+                n_quant(h, u, cols)
+
+        def z4(h, u, ts=ROW4):
+            for t in ts:
+                z_exp(h, u, t)
+
+        def scale4(h, u):
+            for t in ROW4:
+                n_scale(h, u, t)
+
+        def bal4(h, u, e):
+            for c in ROW4:
+                balance(h, u, e, c)
+
+        def balu(h, e, c):
+            for u in range(UNITS):
+                balance(h, u, e, c)
+
+        begin(0)
+        begin(1)
+        with tc.manual_schedule():
+            lam_cast(0, 0)
+            f_move(0)
+            f_scale(0)
+            lam_cast(0, 1)
+            for c in (0, 1):
+                lam_turn(0, c)
+            lam_cast(0, 2)
+            phi_turn(0, 0)
+            phi_turn(0, 1)
+            f_scale(1)
+            lam_mult(0, 0)
+            lam_turn(0, 2)
+            lam_cast(0, 3)
+            lam_mult(0, 1)
+            lam_mult(0, 2)
+            lam_turn(0, 3)
+            phi_copy(0, 0)
+            phi_copy(0, 1)
+            g_lay(0, 0, sc)
+            g_lay(0, 1, sc)
+            lam_mult(0, 3)
+            lam_quant(0, 0)
+            warm_up(6)
+            lam_quant(0, 1)
+            for k in range(LG):
+                for t in ROW4:
+                    z_lam(0, 0, t, k)
+            phi_quant(0)
+            g_quant(0)
+            g_lay(1, 0, sc)
+            g_lay(1, 1, vc)
+            f_move(1)
+            g_quant(1)
+            for t in ROW4:
+                z_phi(0, 0, t)
+                exp(0, 0, t)
+            phi_turn(1, 0)
+            phi_turn(1, 1)
+            phi_copy(1, 0)
+            phi_copy(1, 1)
+            lam_cast(1, 0)
+            g_lay(2, 0, vc)
+            g_lay(2, 1, vc)
+            f_move(2)
+            f_scale(2)
+            g_quant(2)
+            z4(0, 1)
+            lam_cast(1, 1)
+            g_lay(3, 0, vc)
+            g_lay(3, 1, vc)
+            f_move(3)
+            f_scale(3)
+            g_quant(3)
+            z4(0, 2, (0, 1))
+            lam_turn(1, 0)
+            lam_mult(1, 0)
+            lam_cast(1, 2)
+            z4(0, 2, (2, 3))
+            lam_turn(1, 1)
+            lam_mult(1, 1)
+            lam_turn(1, 2)
+            lam_mult(1, 2)
+            lam_cast(1, 3)
+            z4(0, 3, (0, 1))
+            lam_turn(1, 3)
+            lam_mult(1, 3)
+            for k in range(LG):
+                lam_quant(1, k)
+            phi_quant(1)
+            z4(0, 3, (2, 3))
+            n_vector(0, 0)
+            scale4(0, 1)
+            z4(1, 0)
+            n_layq(0, 1)
+            z4(1, 1)
+            scale4(1, 0)
+            n_vector(0, 2)
+            z4(1, 2)
+            scale4(1, 1)
+            n_vector(0, 3)
+            z4(1, 3)
+            n_layq(1, 0)
+            n_layq(1, 1)
+            for c in ROW4:
+                for e in range(2):
+                    balu(0, e, c)
+            finish(0, 0, 0)
+            n_vector(1, 2)
+            n_vector(1, 3)
+            finish(0, 1, 0)
+            for c in (1, 2, 3):
+                for e in range(2):
+                    finish(0, e, c)
+            for c in ROW4:
+                for e in range(2):
+                    balu(1, e, c)
+                    finish(1, e, c, 2 if (c, e) == (3, 1) else 1)

@@ -10,6 +10,7 @@ F32 = mybir.dt.float32
 BF16 = mybir.dt.bfloat16
 U32 = mybir.dt.uint32
 I32 = mybir.dt.int32
+U16 = mybir.dt.uint16
 U8 = mybir.dt.uint8
 FP8 = mybir.dt.float8_e4m3fn
 FP8X4 = mybir.dt.float8_e4m3fn_x4
@@ -22,6 +23,7 @@ HALF = 512
 ROWS = 4
 UNITS = S // 512
 LG = E // 512
+FIRST = 2
 
 
 def tile_equilibrium_mass_balance_s3_kernel(
@@ -32,8 +34,9 @@ def tile_equilibrium_mass_balance_s3_kernel(
         keep = ctx.enter_context(tc.tile_pool(name="keep", bufs=1))
         work = ctx.enter_context(tc.tile_pool(name="work", bufs=2))
         psum = ctx.enter_context(tc.psum_pool(name="psum", bufs=1))
+        ctx.enter_context(tc.manual_schedule())
 
-        lam_v = lam_bytes.rearrange("(h p c) k -> h p c k", h=2, c=ROWS)
+        lam_v = lam_bytes.rearrange("(h p a b) k -> h a p (b k)", h=2, a=2, b=2)
         phi_v = phi.rearrange("(h p c) k -> h p c k", h=2, c=ROWS)
         feed_v = feed.rearrange("(h p c) e -> h p c e", h=2, c=ROWS)
         out_v = out.rearrange("(h p c) e -> h p c e", h=2, c=ROWS)
@@ -41,43 +44,35 @@ def tile_equilibrium_mass_balance_s3_kernel(
         f_v = f_words.rearrange("k p b -> p k b")
         a_v = a_words.rearrange("k p b -> p k b")
 
-        f_sc_raw = keep.tile([P, LG, S], U8, name="f_sc_raw", align_bytes=64)
-        nc.vector.memset(f_sc_raw[:].bitcast(I32), 0)
-        ident = keep.tile([P, P], F32, name="ident")
-        make_identity(nc, ident[:])
-        a_sc = keep.tile([P, UNITS, E], U8, name="a_sc", align_bytes=64)
-        nc.gpsimd.memset(a_sc[:].bitcast(I32), 0)
-        warm = keep.tile([P, 1], F32, name="warm")
-        nc.vector.memset(warm[:], 0.0)
-        nc.scalar.activation(warm[:], warm[:], ACT.Exp)
+        def bank():
+            return psum.tile([P, 512], F32, name="bank", tag="bank", bufs=8)
 
-        lam_sb, phi_sb, feed_sb = [], [], []
-        for h in range(2):
-            t8 = keep.tile([P, ROWS, E], U8, name="lam_sb%d" % h)
-            tb = keep.tile([P, ROWS, D], BF16, name="phi_sb%d" % h)
-            tf = keep.tile([P, ROWS, E], BF16, name="feed_sb%d" % h)
-            lam_sb.append(t8)
-            phi_sb.append(tb)
-            feed_sb.append(tf)
+        lam_sb, phi_sb, feed_sb, g_sb, f_sb, f_raw = {}, {}, {}, {}, {}, {}
 
-        def load_rows(dst, src, h, cs):
-            nc.sync.dma_start(out=dst[h][:, cs, :], in_=src[h][:, cs, :])
+        def load_lam(h, pair):
+            lam_sb[h, pair] = keep.tile([P, 2 * E], U8, name="lam_sb%d%d" % (h, pair))
+            nc.sync.dma_start(out=lam_sb[h, pair][:], in_=lam_v[h, pair])
 
-        g_sb, f_sb = {}, {}
+        def load_phi(h):
+            phi_sb[h] = keep.tile([P, ROWS * D], BF16, name="phi_sb%d" % h)
+            nc.sync.dma_start(out=phi_sb[h][:], in_=phi_v[h].rearrange("p c k -> p (c k)"))
 
-        def load_g(u0, n):
-            t = keep.tile([P, 4, 512 * n], BF16, name="g_sb%d" % u0)
-            nc.sync.dma_start(out=t[:], in_=g_v[:, :, 512 * u0 : 512 * (u0 + n)])
-            for i in range(n):
-                g_sb[u0 + i] = t[:, :, 512 * i : 512 * (i + 1)]
+        def load_feed(h):
+            feed_sb[h] = keep.tile([P, ROWS, E], BF16, name="feed_sb%d" % h)
+            nc.sync.dma_start(out=feed_sb[h][:], in_=feed_v[h])
 
-        def load_f(u0, n):
-            t = keep.tile([P, LG, 1024 * n], U8, name="f_sb%d" % u0)
-            nc.sync.dma_start(out=t[:], in_=f_v[:, :, 1024 * u0 : 1024 * (u0 + n)])
-            for i in range(n):
-                f_sb[u0 + i] = t[:, :, 1024 * i : 1024 * (i + 1)]
+        def load_g(u):
+            g_sb[u] = keep.tile([P, 4, 512], BF16, name="g_sb%d" % u)
+            nc.sync.dma_start(out=g_sb[u][:], in_=g_v[:, :, 512 * u : 512 * (u + 1)])
 
-        a_sb = keep.tile([P, UNITS, 2 * E], U8, name="a_sb", align_bytes=64)
+        def load_f(u):
+            f_sb[u] = keep.tile([P, LG, 1024], U8, name="f_sb%d" % u)
+            nc.sync.dma_start(out=f_sb[u][:], in_=f_v[:, :, 1024 * u : 1024 * (u + 1)])
+
+        def scale_tile(name, passes, width):
+            tile = keep.tile([P, passes, width], U8, name=name, align_bytes=64)
+            nc.vector.memset(tile[:].bitcast(I32), 0)
+            return tile
 
         def load_scales(dst, src):
             rows = src.bitcast(I32).rearrange("k (q r) n -> r q k n", r=4)
@@ -85,137 +80,102 @@ def tile_equilibrium_mass_balance_s3_kernel(
             for r in range(4):
                 nc.sync.dma_start(out=words[r:P:32], in_=rows[r])
 
-        l_sc = keep.tile([P, LG, 4], F32, name="l_sc")
-        m_sb = keep.tile([P, UNITS, 4], BF16, name="m_sb")
-        m_f = keep.tile([P, UNITS * 4], F32, name="m_f")
+        phi_q, phi_s, lam_q, lam_s, phi_t, lam_t, turned, wide = {}, {}, {}, {}, {}, {}, {}, {}
 
-        load_rows(lam_sb, lam_v, 0, slice(0, 2))
-        load_f(0, 1)
-        load_scales(f_sc_raw, f_scales)
-        nc.sync.dma_start(out=l_sc[:], in_=lam_scale.rearrange("o (k p t) -> p (o k) t", p=P, t=4))
-        load_rows(lam_sb, lam_v, 0, slice(2, 4))
-        load_rows(phi_sb, phi_v, 0, slice(0, 4))
-        load_g(0, 1)
-        load_f(1, 1)
-        load_g(1, 1)
-        load_rows(phi_sb, phi_v, 1, slice(0, 4))
-        nc.sync.dma_start(out=m_sb[:], in_=m.rearrange("(u p t) -> p u t", p=P, t=4))
-        nc.gpsimd.tensor_copy(out=m_f[:], in_=m_sb[:].rearrange("p u t -> p (u t)"))
-        load_f(2, 2)
-        load_g(2, 2)
-        load_rows(lam_sb, lam_v, 1, slice(0, 4))
-        load_scales(a_sc, a_scales)
-        nc.sync.dma_start(out=a_sb[:], in_=a_v)
-        for h in range(2):
-            load_rows(feed_sb, feed_v, h, slice(0, 4))
+        def lam_cast(h, k, c, eng):
+            if (h, k) not in wide:
+                wide[h, k] = work.tile([P, ROWS * 512], BF16, name="wide", tag="wide", bufs=2)
+            at = E * (c % 2) + 512 * k
+            copy = nc.scalar.copy if eng == "s" else nc.vector.tensor_copy
+            copy(wide[h, k][:, 512 * c : 512 * (c + 1)], lam_sb[h, c // 2][:, at : at + 512].bitcast(FP8))
 
-        phi_q, phi_s, lam_q, lam_s, phi_t, lam_t, tps, casts = {}, {}, {}, {}, {}, {}, {}, {}
-
-        def begin(h):
-            phi_t[h] = work.tile([P, HALF, 4], BF16, name="phi_t", tag="phi_t", bufs=2, align_bytes=64)
-            phi_q[h] = keep.tile([P, HALF], U32, name="phi_q%d" % h, align_bytes=64)
-            phi_s[h] = keep.tile([P, HALF], U8, name="phi_s%d" % h, align_bytes=64)
-            lam_t[h] = work.tile([P, LG, HALF, 4], BF16, name="lam_t", tag="lam_t", bufs=1, align_bytes=64)
-            lam_q[h] = keep.tile([P, LG, HALF], U32, name="lam_q%d" % h, align_bytes=64)
-            lam_s[h] = keep.tile([P, LG, HALF], U8, name="lam_s%d" % h, align_bytes=64)
-
-        def phi_turn(h, pair):
-            tps[h, "p", pair] = psum.tile([P, 512], F32, name="tp", tag="acc", bufs=4)
+        def turn(key, rows, pair):
+            turned[key] = bank()
+            words = rows.bitcast(F32)
             for i in range(2):
-                words = phi_sb[h][:, 2 * pair + i, :].bitcast(F32)
+                c = 2 * pair + i
                 for u in range(2):
-                    k = 128 * (2 * i + u)
-                    nc.tensor.transpose(tps[h, "p", pair][:, k : k + 128], words[:, u::2], ident[:])
-
-        def phi_copy(h, pair):
-            dst = phi_t[h][:].rearrange("p r t -> p (r t)").bitcast(F32)
-            dst = dst.rearrange("p (c r u) -> p c r u", c=4, u=2)
-            nc.scalar.copy(
-                dst[:, 2 * pair : 2 * pair + 2], tps[h, "p", pair][:].rearrange("p (c u r) -> p c r u", c=2, u=2)
-            )
-
-        def phi_quant(h):
-            nc.vector.quantize_mx(
-                out=phi_q[h][:].bitcast(FP8X4), scales=phi_s[h][:], in_=phi_t[h][:].rearrange("p r t -> p (r t)")
-            )
-
-        def lam_cast(h, c):
-            casts[h, c] = work.tile([P, E], BF16, name="cast", tag="cast", bufs=3)
-            nc.scalar.copy(casts[h, c][:], lam_sb[h][:, c, :].bitcast(FP8))
-
-        def lam_turn(h, c):
-            words = casts[h, c][:].bitcast(F32)
-            tps[h, c] = psum.tile([P, 512], F32, name="tp", tag="acc", bufs=4)
-            for k in range(LG):
-                for u in range(2):
-                    b = 128 * (2 * k + u)
+                    at = 256 * u + 128 * i
                     nc.tensor.transpose(
-                        tps[h, c][:, b : b + 128], words[:, 256 * k + u : 256 * (k + 1) : 2], ident[:]
+                        turned[key][:, at : at + 128], words[:, 256 * c + u : 256 * (c + 1) : 2], ident[:]
                     )
 
-        def lam_mult(h, c):
-            for k in range(LG):
-                vals = tps[h, c][:, 256 * k : 256 * (k + 1)].bitcast(BF16)
-                nc.vector.tensor_tensor(
-                    out=lam_t[h][:, k, 128 * c : 128 * (c + 1), :].rearrange("p r (u e) -> p r u e", e=2),
-                    in0=vals.rearrange("p (u r e) -> p r u e", u=2, e=2),
-                    in1=l_sc[:, k, :].rearrange("p (u e) -> p u e", e=2).unsqueeze(1).to_broadcast([P, P, 2, 2]),
-                    op=ALU.mult,
-                )
+        def lam_turn(h, k, pair):
+            turn((h, k, pair), wide[h, k][:], pair)
+
+        def phi_turn(h, pair):
+            turn((h, "phi", pair), phi_sb[h][:], pair)
+
+        def lam_mult(h, k, pair):
+            if pair == 0:
+                lam_t[h, k] = work.tile([P, HALF, 4], BF16, name="lam_t", tag="lam_t", bufs=2, align_bytes=64)
+            nc.vector.tensor_tensor(
+                out=lam_t[h, k][:, 256 * pair : 256 * (pair + 1), :].rearrange("p r (u e) -> p r u e", e=2),
+                in0=turned[h, k, pair][:].bitcast(BF16).rearrange("p (u r e) -> p r u e", u=2, e=2),
+                in1=l_sc[:, k, :].rearrange("p (u e) -> p u e", e=2).unsqueeze(1).to_broadcast([P, 256, 2, 2]),
+                op=ALU.mult,
+            )
+
+        def phi_copy(h, pair):
+            if pair == 0:
+                phi_t[h] = work.tile([P, HALF, 4], BF16, name="phi_t", tag="phi_t", bufs=1, align_bytes=64)
+            dst = phi_t[h][:].rearrange("p r t -> p (r t)").bitcast(F32).rearrange("p (r u) -> p r u", u=2)
+            nc.scalar.copy(
+                dst[:, 256 * pair : 256 * (pair + 1)], turned[h, "phi", pair][:].rearrange("p (u r) -> p r u", u=2)
+            )
+
+        def quantise(name, src):
+            codes = keep.tile([P, 512], U32, name=name + "_q", align_bytes=64)
+            scales = keep.tile([P, 512], U8, name=name + "_s", align_bytes=64)
+            nc.vector.quantize_mx(out=codes[:].bitcast(FP8X4), scales=scales[:], in_=src[:].rearrange("p r t -> p (r t)"))
+            return codes, scales
+
+        def phi_quant(h):
+            phi_q[h], phi_s[h] = quantise("phi%d" % h, phi_t[h])
 
         def lam_quant(h, k):
-            nc.vector.quantize_mx(
-                out=lam_q[h][:, k, :].bitcast(FP8X4),
-                scales=lam_s[h][:, k, :],
-                in_=lam_t[h][:, k].rearrange("p r t -> p (r t)"),
-            )
+            lam_q[h, k], lam_s[h, k] = quantise("lam%d%d" % (h, k), lam_t[h, k])
 
         g_q, g_s, f_p, f_sp, g_i = {}, {}, {}, {}, {}
 
-        def g_lay(u, i, copy):
+        def g_lay(u, i, eng):
             if u not in g_i:
                 g_i[u] = work.tile([P, 512, 4], BF16, name="gi", tag="gi", bufs=2, align_bytes=64)
-            ms = slice(64 * i, 64 * i + 64)
+            ms = slice(32 * i, 32 * i + 32)
+            copy = nc.scalar.copy if eng == "s" else nc.vector.tensor_copy
             copy(
-                g_i[u][:].rearrange("p (t m) j -> p m t j", t=4)[:, ms],
-                g_sb[u].rearrange("p j (m t) -> p m t j", t=4)[:, ms],
+                g_i[u][:].rearrange("p (t a b) j -> p a j b t", t=4, b=2)[:, ms],
+                g_sb[u][:].rearrange("p j (a b t) -> p a j b t", t=4, b=2)[:, ms],
             )
 
         def g_quant(u):
-            g_q[u] = keep.tile([P, 512], U32, name="g_q%d" % u, align_bytes=64)
-            g_s[u] = keep.tile([P, 512], U8, name="g_s%d" % u, align_bytes=64)
-            nc.vector.quantize_mx(
-                out=g_q[u][:].bitcast(FP8X4), scales=g_s[u][:], in_=g_i[u][:].rearrange("p s j -> p (s j)")
-            )
+            g_q[u], g_s[u] = quantise("g%d" % u, g_i[u])
 
         def f_move(u):
             f_p[u] = keep.tile([P, LG, 1024], U8, name="f_p%d" % u, align_bytes=64)
-            for k in range(LG):
-                nc.vector.tensor_copy(
-                    out=f_p[u][:, k, :].rearrange("p (t m b) -> p t m b", t=4, b=2),
-                    in_=f_sb[u][:, k, :].rearrange("p (m t b) -> p t m b", t=4, b=2),
-                )
+            nc.vector.tensor_copy(
+                out=f_p[u][:].bitcast(U16).rearrange("p k (t m) -> p k t m", t=4),
+                in_=f_sb[u][:].bitcast(U16).rearrange("p k (m t) -> p k t m", t=4),
+            )
 
         def f_scale(u):
             f_sp[u] = keep.tile([P, LG, 512], U8, name="f_sp%d" % u, align_bytes=64)
             nc.vector.tensor_copy(
                 out=f_sp[u][:].rearrange("p k (t m) -> p k t m", t=4),
-                in_=f_sc_raw[:, :, 512 * u : 512 * (u + 1)].rearrange("p k (m t) -> p k t m", t=4),
+                in_=f_raw[u].rearrange("p k (m t) -> p k t m", t=4),
             )
 
-        e_sb, flat, nb, n_q, n_s = {}, {}, {}, {}, {}
-
-        z_ps = {}
+        e_sb, flat, nb, n_q, n_s, z_ps = {}, {}, {}, {}, {}, {}
 
         def z_lam(h, u, t, k):
             if k == 0:
-                z_ps[h, u, t] = psum.tile([P, HALF], F32, name="zp", tag="z", bufs=4)
+                z_ps[h, u, t] = bank()
             nc.tensor.matmul_mx(
                 out=z_ps[h, u, t][:],
                 lhsT=f_p[u][:, k, 256 * t : 256 * (t + 1)].bitcast(FP4X4),
                 lhsT_scale=f_sp[u][:, k, 128 * t : 128 * (t + 1)],
-                rhs=lam_q[h][:, k, :].bitcast(FP8X4),
-                rhs_scale=lam_s[h][:, k, :],
+                rhs=lam_q[h, k][:].bitcast(FP8X4),
+                rhs_scale=lam_s[h, k][:],
                 start=(k == 0), stop=False,
             )
 
@@ -228,19 +188,8 @@ def tile_equilibrium_mass_balance_s3_kernel(
 
         def exp(h, u, t):
             if t == 0:
-                e_sb[h, u] = work.tile([P, 4, HALF], F32, name="e_sb", tag="e_sb", bufs=5)
+                e_sb[h, u] = work.tile([P, 4, HALF], F32, name="e_sb", tag="e_sb", bufs=6)
             nc.scalar.activation(e_sb[h, u][:, t, :], z_ps[h, u, t][:], ACT.Exp)
-
-        def z_exp(h, u, t):
-            for k in range(LG):
-                z_lam(h, u, t, k)
-            z_phi(h, u, t)
-            exp(h, u, t)
-
-        def n_begin(h, u):
-            nb[h, u] = work.tile([P, HALF, 4], BF16, name="nb", tag="nb", bufs=2, align_bytes=64)
-            n_q[h, u] = keep.tile([P, HALF], U32, name="n_q%d%d" % (h, u), align_bytes=64)
-            n_s[h, u] = keep.tile([P, HALF], U8, name="n_s%d%d" % (h, u), align_bytes=64)
 
         def n_scale(h, u, t):
             if t == 0:
@@ -249,191 +198,228 @@ def tile_equilibrium_mass_balance_s3_kernel(
                 flat[h, u][:, t, :], e_sb[h, u][:, t, :], ACT.Copy, scale=m_f[:, 4 * u + t : 4 * u + t + 1]
             )
 
-        def n_lay(h, u, cols):
+        def n_lay(h, u):
+            nb[h, u] = work.tile([P, HALF, 4], BF16, name="nb", tag="nb", bufs=2, align_bytes=64)
             nc.vector.tensor_copy(
-                out=nb[h, u][:, cols, :].rearrange("p (r i) t -> p r t i", i=4),
-                in_=flat[h, u][:, :, cols].rearrange("p t (r i) -> p r t i", i=4),
+                out=nb[h, u][:].rearrange("p (r i) t -> p r t i", i=4),
+                in_=flat[h, u][:].rearrange("p t (r i) -> p r t i", i=4),
             )
 
-        def n_mult(h, u, cols):
+        def n_mult(h, u):
+            nb[h, u] = work.tile([P, HALF, 4], BF16, name="nb", tag="nb", bufs=2, align_bytes=64)
             nc.vector.tensor_tensor(
-                out=nb[h, u][:, cols, :].rearrange("p (r i) t -> p r t i", i=4),
-                in0=e_sb[h, u][:, :, cols].rearrange("p t (r i) -> p r t i", i=4),
-                in1=m_sb[:, u, :].unsqueeze(1).unsqueeze(3).to_broadcast([P, (cols.stop - cols.start) // 4, 4, 4]),
+                out=nb[h, u][:].rearrange("p (r i) t -> p r t i", i=4),
+                in0=e_sb[h, u][:].rearrange("p t (r i) -> p r t i", i=4),
+                in1=m_f[:, 4 * u : 4 * u + 4].unsqueeze(1).unsqueeze(3).to_broadcast([P, HALF // 4, 4, 4]),
                 op=ALU.mult,
             )
 
-        def n_quant(h, u, cols):
-            nc.vector.quantize_mx(
-                out=n_q[h, u][:, cols].bitcast(FP8X4),
-                scales=n_s[h, u][:, cols],
-                in_=nb[h, u][:, cols, :].rearrange("p r t -> p (r t)"),
-            )
+        def n_quant(h, u):
+            n_q[h, u], n_s[h, u] = quantise("n%d%d" % (h, u), nb[h, u])
 
         acc = {}
 
-        def balance(h, u, e, c):
-            if u == 0:
-                tag = ("acc", 4) if e == 0 else ("z", 4)
-                acc[h, c, e] = psum.tile([P, 512], F32, name="ac", tag=tag[0], bufs=tag[1])
+        def balance(h, c, e):
+            acc[h, c, e] = bank()
             cols = slice(128 * c, 128 * (c + 1))
-            nc.tensor.matmul_mx(
-                out=acc[h, c, e][:],
-                lhsT=n_q[h, u][:, cols].bitcast(FP8X4), lhsT_scale=n_s[h, u][:, cols],
-                rhs=a_sb[:, u, 1024 * e : 1024 * (e + 1)].bitcast(FP4X4),
-                rhs_scale=a_sc[:, u, 512 * e : 512 * (e + 1)],
-                start=(u == 0), stop=(u == UNITS - 1),
-            )
+            for u in range(UNITS):
+                nc.tensor.matmul_mx(
+                    out=acc[h, c, e][:],
+                    lhsT=n_q[h, u][:, cols].bitcast(FP8X4), lhsT_scale=n_s[h, u][:, cols],
+                    rhs=a_sb[:, u, 1024 * e : 1024 * (e + 1)].bitcast(FP4X4),
+                    rhs_scale=a_sc[:, u, 512 * e : 512 * (e + 1)],
+                    start=(u == 0), stop=(u == UNITS - 1),
+                )
 
-        def finish(h, e, c, parts=1):
+        def finish(h, c, e, parts=1):
             w = 512 // parts
             for i in range(parts):
                 cols = slice(512 * e + w * i, 512 * e + w * (i + 1))
-                o = work.tile([P, w], F32, name="o", tag="o", bufs=8)
+                o = work.tile([P, w], F32, name="o", tag="o", bufs=5)
                 nc.vector.tensor_tensor(
                     out=o[:], in0=acc[h, c, e][:, w * i : w * (i + 1)], in1=feed_sb[h][:, c, cols], op=ALU.subtract
                 )
                 nc.sync.dma_start(out=out_v[h][:, c, cols], in_=o[:])
 
-        def warm_up(n):
-            wp = psum.tile([P, 512], F32, name="wp", tag="acc", bufs=4)
-            for i in range(n):
-                nc.tensor.matmul(
-                    wp[:], lhsT=phi_sb[0][:, 0, 0:P], rhs=phi_sb[0][:, 0, :], start=True, stop=True
-                )
+        FOUR = range(4)
 
-        ROW4 = range(4)
-        halves = [slice(0, 256), slice(256, 512)]
-        quarters = [slice(128 * c, 128 * c + 128) for c in ROW4]
-        vc, sc = nc.vector.tensor_copy, nc.scalar.copy
+        def z_lams(h, u, k):
+            for t in FOUR:
+                z_lam(h, u, t, k)
 
-        def n_vector(h, u):
-            n_begin(h, u)
-            for cols in halves:
-                n_mult(h, u, cols)
-            for cols in halves:
-                n_quant(h, u, cols)
+        def z_tile(h, u, t):
+            for k in range(LG):
+                z_lam(h, u, t, k)
+            z_phi(h, u, t)
+            exp(h, u, t)
 
-        def n_layq(h, u):
-            n_begin(h, u)
-            for cols in halves:
-                n_lay(h, u, cols)
-            for cols in halves:
-                n_quant(h, u, cols)
+        def z_unit(h, u):
+            for t in FOUR:
+                z_tile(h, u, t)
 
-        def z4(h, u, ts=ROW4):
-            for t in ts:
-                z_exp(h, u, t)
-
-        def scale4(h, u):
-            for t in ROW4:
+        def scale_unit(h, u):
+            for t in FOUR:
                 n_scale(h, u, t)
 
-        def bal4(h, u, e):
-            for c in ROW4:
-                balance(h, u, e, c)
 
-        def balu(h, e, c):
-            for u in range(UNITS):
-                balance(h, u, e, c)
+        f_first = scale_tile("f_first", LG, 512 * FIRST)
+        ident = keep.tile([P, P], F32, name="ident")
+        make_identity(nc, ident[:])
+        f_rest = scale_tile("f_rest", LG, S - 512 * FIRST)
+        for u in range(UNITS):
+            src, at = (f_first, u) if u < FIRST else (f_rest, u - FIRST)
+            f_raw[u] = src[:, :, 512 * at : 512 * (at + 1)]
+        a_sc = scale_tile("a_sc", UNITS, E)
+        l_sc = keep.tile([P, LG, 4], F32, name="l_sc")
+        m_sb = keep.tile([P, UNITS, 4], BF16, name="m_sb")
+        m_f = keep.tile([P, UNITS * 4], F32, name="m_f")
+        a_sb = keep.tile([P, UNITS, 2 * E], U8, name="a_sb", align_bytes=64)
 
-        begin(0)
-        begin(1)
-        with tc.manual_schedule():
-            lam_cast(0, 0)
-            f_move(0)
-            f_scale(0)
-            lam_cast(0, 1)
-            for c in (0, 1):
-                lam_turn(0, c)
-            lam_cast(0, 2)
-            phi_turn(0, 0)
-            phi_turn(0, 1)
-            f_scale(1)
-            lam_mult(0, 0)
-            lam_turn(0, 2)
-            lam_cast(0, 3)
-            lam_mult(0, 1)
-            lam_mult(0, 2)
-            lam_turn(0, 3)
-            phi_copy(0, 0)
-            phi_copy(0, 1)
-            g_lay(0, 0, sc)
-            g_lay(0, 1, sc)
-            lam_mult(0, 3)
-            lam_quant(0, 0)
-            warm_up(6)
-            lam_quant(0, 1)
-            for k in range(LG):
-                for t in ROW4:
-                    z_lam(0, 0, t, k)
-            phi_quant(0)
-            g_quant(0)
-            g_lay(1, 0, sc)
-            g_lay(1, 1, vc)
-            f_move(1)
-            g_quant(1)
-            for t in ROW4:
-                z_phi(0, 0, t)
-                exp(0, 0, t)
-            phi_turn(1, 0)
-            phi_turn(1, 1)
-            phi_copy(1, 0)
-            phi_copy(1, 1)
-            lam_cast(1, 0)
-            g_lay(2, 0, vc)
-            g_lay(2, 1, vc)
-            f_move(2)
-            f_scale(2)
-            g_quant(2)
-            z4(0, 1)
-            lam_cast(1, 1)
-            g_lay(3, 0, vc)
-            g_lay(3, 1, vc)
-            f_move(3)
-            f_scale(3)
-            g_quant(3)
-            z4(0, 2, (0, 1))
-            lam_turn(1, 0)
-            lam_mult(1, 0)
-            lam_cast(1, 2)
-            z4(0, 2, (2, 3))
-            lam_turn(1, 1)
-            lam_mult(1, 1)
-            lam_turn(1, 2)
-            lam_mult(1, 2)
-            lam_cast(1, 3)
-            z4(0, 3, (0, 1))
-            lam_turn(1, 3)
-            lam_mult(1, 3)
-            for k in range(LG):
-                lam_quant(1, k)
-            phi_quant(1)
-            z4(0, 3, (2, 3))
-            n_vector(0, 0)
-            scale4(0, 1)
-            z4(1, 0)
-            n_layq(0, 1)
-            z4(1, 1)
-            scale4(1, 0)
-            n_vector(0, 2)
-            z4(1, 2)
-            scale4(1, 1)
-            n_vector(0, 3)
-            z4(1, 3)
-            n_layq(1, 0)
-            n_layq(1, 1)
-            for c in ROW4:
-                for e in range(2):
-                    balu(0, e, c)
-            finish(0, 0, 0)
-            n_vector(1, 2)
-            n_vector(1, 3)
-            finish(0, 1, 0)
-            for c in (1, 2, 3):
-                for e in range(2):
-                    finish(0, e, c)
-            for c in ROW4:
-                for e in range(2):
-                    balu(1, e, c)
-                    finish(1, e, c, 2 if (c, e) == (3, 1) else 1)
+        load_lam(0, 0)
+        nc.sync.dma_start(out=l_sc[:], in_=lam_scale.rearrange("o (k p t) -> p (o k) t", p=P, t=4))
+        load_f(0)
+        load_lam(0, 1)
+        load_scales(f_first, f_scales[:, :, : 512 * FIRST])
+        load_phi(0)
+        load_g(0)
+        load_f(1)
+        load_g(1)
+        load_scales(f_rest, f_scales[:, :, 512 * FIRST :])
+        load_f(2)
+        load_g(2)
+        load_lam(1, 0)
+        load_lam(1, 1)
+        load_f(3)
+        load_g(3)
+        nc.sync.dma_start(out=m_sb[:], in_=m.rearrange("(u p t) -> p u t", p=P, t=4))
+        load_phi(1)
+        load_scales(a_sc, a_scales)
+        nc.sync.dma_start(out=a_sb[:], in_=a_v)
+        load_feed(0)
+        load_feed(1)
+
+        lam_cast(0, 0, 0, "v")
+        lam_cast(0, 0, 1, "s")
+        lam_turn(0, 0, 0)
+        lam_cast(0, 1, 0, "s")
+        lam_cast(0, 1, 1, "s")
+        lam_turn(0, 1, 0)
+        f_move(0)
+        lam_cast(0, 0, 2, "s")
+        lam_cast(0, 0, 3, "s")
+        lam_mult(0, 0, 0)
+        lam_turn(0, 0, 1)
+        lam_cast(0, 1, 2, "s")
+        lam_cast(0, 1, 3, "s")
+        lam_mult(0, 1, 0)
+        lam_mult(0, 0, 1)
+        phi_turn(0, 0)
+        phi_turn(0, 1)
+        lam_turn(0, 1, 1)
+        f_scale(0)
+        lam_quant(0, 0)
+        phi_copy(0, 0)
+        phi_copy(0, 1)
+        z_lams(0, 0, 0)
+        lam_mult(0, 1, 1)
+        g_lay(0, 0, "s")
+        g_lay(0, 1, "s")
+        phi_quant(0)
+        lam_quant(0, 1)
+        g_quant(0)
+        z_lams(0, 0, 1)
+        g_lay(1, 0, "s")
+        g_lay(1, 1, "s")
+        f_move(1)
+        f_scale(1)
+        for t in FOUR:
+            z_phi(0, 0, t)
+            exp(0, 0, t)
+        z_lams(0, 1, 0)
+        z_lams(0, 1, 1)
+        f_move(2)
+        g_quant(1)
+        f_scale(2)
+        for t in FOUR:
+            z_phi(0, 1, t)
+        g_lay(2, 0, "v")
+        g_lay(2, 1, "v")
+        for c in FOUR:
+            lam_cast(1, 1, c, "s")
+        f_move(3)
+        g_quant(2)
+        for t in FOUR:
+            exp(0, 1, t)
+        for c in FOUR:
+            lam_cast(1, 0, c, "v")
+        z_lams(0, 2, 0)
+        z_lams(0, 2, 1)
+        f_scale(3)
+        g_lay(3, 0, "v")
+        g_lay(3, 1, "v")
+        for t in FOUR:
+            z_phi(0, 2, t)
+            exp(0, 2, t)
+        nc.vector.tensor_copy(out=m_f[:], in_=m_sb[:].rearrange("p u t -> p (u t)"))
+        g_quant(3)
+        for k in range(LG):
+            lam_turn(1, k, 0)
+            lam_turn(1, k, 1)
+        lam_mult(1, 0, 0)
+        lam_mult(1, 0, 1)
+        scale_unit(0, 0)
+        z_unit(0, 3)
+        lam_mult(1, 1, 0)
+        lam_quant(1, 0)
+        lam_mult(1, 1, 1)
+        phi_turn(1, 0)
+        phi_turn(1, 1)
+        phi_copy(1, 0)
+        phi_copy(1, 1)
+        lam_quant(1, 1)
+        n_lay(0, 0)
+        scale_unit(0, 1)
+        z_lams(1, 0, 0)
+        z_lams(1, 0, 1)
+        phi_quant(1)
+        n_quant(0, 0)
+        n_mult(0, 2)
+        for t in FOUR:
+            z_phi(1, 0, t)
+            exp(1, 0, t)
+        n_lay(0, 1)
+        n_quant(0, 2)
+        z_unit(1, 1)
+        n_quant(0, 1)
+        n_mult(0, 3)
+        for t in FOUR:
+            z_tile(1, 2, t)
+            n_scale(1, 1, t)
+        n_mult(1, 0)
+        n_quant(0, 3)
+        for t in FOUR:
+            z_tile(1, 3, t)
+            n_scale(1, 2, t)
+        n_lay(1, 1)
+        n_quant(1, 0)
+        scale_unit(1, 3)
+        for c in FOUR:
+            for e in range(2):
+                balance(0, c, e)
+        n_lay(1, 2)
+        n_quant(1, 1)
+        finish(0, 0, 0)
+        n_quant(1, 2)
+        finish(0, 0, 1)
+        n_lay(1, 3)
+        finish(0, 1, 0)
+        n_quant(1, 3)
+        finish(0, 1, 1)
+        finish(0, 2, 0)
+        finish(0, 2, 1)
+        finish(0, 3, 0)
+        finish(0, 3, 1)
+        for c in FOUR:
+            for e in range(2):
+                balance(1, c, e)
+                finish(1, c, e, 2 if (c, e) == (3, 1) else 1)

@@ -100,6 +100,27 @@ def tile_equilibrium_mass_balance_s3_kernel(
                         turned[key][:, at : at + 128], words[:, 256 * c + u : 256 * (c + 1) : 2], ident[:]
                     )
 
+        def lam_spread(h, pair):
+            wide[h, "p", pair] = work.tile([P, 2 * E], BF16, name="wide", tag="wide", bufs=2)
+            nc.vector.tensor_scalar(
+                out=wide[h, "p", pair][:].rearrange("p (u w e) -> p w u e", u=2, e=2),
+                in0=lam_sb[h, pair][:].bitcast(FP8).rearrange("p (w u e) -> p w u e", u=2, e=2),
+                scalar1=one[:], scalar2=None, op0=ALU.mult,
+            )
+
+        def lam_turn_whole(h, k, pair):
+            turned[h, k, pair] = bank()
+            words = wide[h, "p", pair][:].bitcast(F32)
+            for i in range(2):
+                for u in range(2):
+                    at, src = 256 * u + 128 * i, 512 * u + 256 * i + 128 * k
+                    nc.tensor.transpose(turned[h, k, pair][:, at : at + 128], words[:, src : src + 128], ident[:])
+
+        def warm_up(n):
+            wp = bank()
+            for i in range(n):
+                nc.tensor.matmul(wp[:], lhsT=phi_sb[0][:, 0:P], rhs=phi_sb[0][:, 0:512], start=True, stop=True)
+
         def lam_turn(h, k, pair):
             turn((h, k, pair), wide[h, k][:], pair)
 
@@ -151,16 +172,16 @@ def tile_equilibrium_mass_balance_s3_kernel(
         def g_quant(u):
             g_q[u], g_s[u] = quantise("g%d" % u, g_i[u])
 
-        def f_move(u):
+        def f_move(u, eng="v"):
             f_p[u] = keep.tile([P, LG, 1024], U8, name="f_p%d" % u, align_bytes=64)
-            nc.vector.tensor_copy(
+            (nc.gpsimd if eng == "g" else nc.vector).tensor_copy(
                 out=f_p[u][:].bitcast(U16).rearrange("p k (t m) -> p k t m", t=4),
                 in_=f_sb[u][:].bitcast(U16).rearrange("p k (m t) -> p k t m", t=4),
             )
 
-        def f_scale(u):
+        def f_scale(u, eng="v"):
             f_sp[u] = keep.tile([P, LG, 512], U8, name="f_sp%d" % u, align_bytes=64)
-            nc.vector.tensor_copy(
+            (nc.gpsimd if eng == "g" else nc.vector).tensor_copy(
                 out=f_sp[u][:].rearrange("p k (t m) -> p k t m", t=4),
                 in_=f_raw[u].rearrange("p k (m t) -> p k t m", t=4),
             )
@@ -274,6 +295,8 @@ def tile_equilibrium_mass_balance_s3_kernel(
         m_sb = keep.tile([P, UNITS, 4], BF16, name="m_sb")
         m_f = keep.tile([P, UNITS * 4], F32, name="m_f")
         a_sb = keep.tile([P, UNITS, 2 * E], U8, name="a_sb", align_bytes=64)
+        one = keep.tile([P, 1], F32, name="one")
+        nc.vector.memset(one[:], 1.0)
 
         load_lam(0, 0)
         nc.sync.dma_start(out=l_sc[:], in_=lam_scale.rearrange("o (k p t) -> p (o k) t", p=P, t=4))
@@ -342,16 +365,14 @@ def tile_equilibrium_mass_balance_s3_kernel(
         f_scale(2)
         for t in FOUR:
             z_phi(0, 1, t)
-        g_lay(2, 0, "v")
-        g_lay(2, 1, "v")
-        for c in FOUR:
-            lam_cast(1, 1, c, "s")
+        g_lay(2, 0, "s")
+        g_lay(2, 1, "s")
+        lam_spread(1, 0)
+        lam_spread(1, 1)
         f_move(3)
         g_quant(2)
         for t in FOUR:
             exp(0, 1, t)
-        for c in FOUR:
-            lam_cast(1, 0, c, "v")
         z_lams(0, 2, 0)
         z_lams(0, 2, 1)
         f_scale(3)
@@ -363,62 +384,58 @@ def tile_equilibrium_mass_balance_s3_kernel(
         nc.vector.tensor_copy(out=m_f[:], in_=m_sb[:].rearrange("p u t -> p (u t)"))
         g_quant(3)
         for k in range(LG):
-            lam_turn(1, k, 0)
-            lam_turn(1, k, 1)
+            lam_turn_whole(1, k, 0)
+            lam_turn_whole(1, k, 1)
+        phi_turn(1, 0)
+        phi_turn(1, 1)
         lam_mult(1, 0, 0)
         lam_mult(1, 0, 1)
-        scale_unit(0, 0)
-        z_unit(0, 3)
+        phi_copy(1, 0)
+        phi_copy(1, 1)
+        for t in FOUR:
+            z_tile(0, 3, t)
+            n_scale(0, 0, t)
         lam_mult(1, 1, 0)
         lam_quant(1, 0)
         lam_mult(1, 1, 1)
-        phi_turn(1, 0)
-        phi_turn(1, 1)
-        phi_copy(1, 0)
-        phi_copy(1, 1)
+        phi_quant(1)
         lam_quant(1, 1)
+        n_mult(0, 2)
         n_lay(0, 0)
-        scale_unit(0, 1)
         z_lams(1, 0, 0)
         z_lams(1, 0, 1)
-        phi_quant(1)
-        n_quant(0, 0)
-        n_mult(0, 2)
         for t in FOUR:
             z_phi(1, 0, t)
+            n_scale(0, 1, t)
             exp(1, 0, t)
-        n_lay(0, 1)
         n_quant(0, 2)
-        z_unit(1, 1)
-        n_quant(0, 1)
         n_mult(0, 3)
+        n_quant(0, 0)
+        z_unit(1, 1)
+        n_lay(0, 1)
+        n_quant(0, 3)
+        n_mult(1, 0)
+        n_quant(0, 1)
         for t in FOUR:
             z_tile(1, 2, t)
             n_scale(1, 1, t)
-        n_mult(1, 0)
-        n_quant(0, 3)
-        for t in FOUR:
-            z_tile(1, 3, t)
-            n_scale(1, 2, t)
+        z_unit(1, 3)
+        scale_unit(1, 2)
         n_lay(1, 1)
         n_quant(1, 0)
-        scale_unit(1, 3)
         for c in FOUR:
             for e in range(2):
                 balance(0, c, e)
-        n_lay(1, 2)
-        n_quant(1, 1)
         finish(0, 0, 0)
-        n_quant(1, 2)
-        finish(0, 0, 1)
-        n_lay(1, 3)
-        finish(0, 1, 0)
+        n_quant(1, 1)
+        n_mult(1, 3)
+        n_lay(1, 2)
         n_quant(1, 3)
-        finish(0, 1, 1)
-        finish(0, 2, 0)
-        finish(0, 2, 1)
-        finish(0, 3, 0)
-        finish(0, 3, 1)
+        finish(0, 0, 1)
+        n_quant(1, 2)
+        for c in (1, 2, 3):
+            for e in range(2):
+                finish(0, c, e)
         for c in FOUR:
             for e in range(2):
                 balance(1, c, e)

@@ -339,6 +339,7 @@ def tile_equilibrium_mass_balance_s3_kernel(
         phi_turn(0, 0)
         phi_turn(0, 1)
         lam_turn(0, 1, 1)
+        warm_up(3)
         f_scale(0)
         lam_quant(0, 0)
         phi_copy(0, 0)

@@ -24,6 +24,7 @@ ROWS = 4
 UNITS = S // 512
 LG = E // 512
 FIRST = 2
+PHB = 1
 
 
 def tile_equilibrium_mass_balance_s3_kernel(
@@ -139,7 +140,7 @@ def tile_equilibrium_mass_balance_s3_kernel(
 
         def phi_copy(h, pair):
             if pair == 0:
-                phi_t[h] = work.tile([P, HALF, 4], BF16, name="phi_t", tag="phi_t", bufs=1, align_bytes=64)
+                phi_t[h] = work.tile([P, HALF, 4], BF16, name="phi_t", tag="phi_t", bufs=PHB, align_bytes=64)
             dst = phi_t[h][:].rearrange("p r t -> p (r t)").bitcast(F32).rearrange("p (r u) -> p r u", u=2)
             nc.scalar.copy(
                 dst[:, 256 * pair : 256 * (pair + 1)], turned[h, "phi", pair][:].rearrange("p (u r) -> p r u", u=2)
@@ -179,17 +180,19 @@ def tile_equilibrium_mass_balance_s3_kernel(
                 in_=f_sb[u][:].bitcast(U16).rearrange("p k (m t) -> p k t m", t=4),
             )
 
-        def f_scale(u, eng="v"):
-            f_sp[u] = keep.tile([P, LG, 512], U8, name="f_sp%d" % u, align_bytes=64)
+        def f_scale(u, ks=range(LG), eng="v"):
+            if u not in f_sp:
+                f_sp[u] = keep.tile([P, LG, 512], U8, name="f_sp%d" % u, align_bytes=64)
+            ks = slice(ks[0], ks[-1] + 1)
             (nc.gpsimd if eng == "g" else nc.vector).tensor_copy(
-                out=f_sp[u][:].rearrange("p k (t m) -> p k t m", t=4),
-                in_=f_raw[u].rearrange("p k (m t) -> p k t m", t=4),
+                out=f_sp[u][:, ks].rearrange("p k (t m) -> p k t m", t=4),
+                in_=f_raw[u][:, ks].rearrange("p k (m t) -> p k t m", t=4),
             )
 
         e_sb, flat, nb, n_q, n_s, z_ps = {}, {}, {}, {}, {}, {}
 
-        def z_lam(h, u, t, k):
-            if k == 0:
+        def z_lam(h, u, t, k, phi_first=False):
+            if k == 0 and not phi_first:
                 z_ps[h, u, t] = bank()
             nc.tensor.matmul_mx(
                 out=z_ps[h, u, t][:],
@@ -197,14 +200,16 @@ def tile_equilibrium_mass_balance_s3_kernel(
                 lhsT_scale=f_sp[u][:, k, 128 * t : 128 * (t + 1)],
                 rhs=lam_q[h, k][:].bitcast(FP8X4),
                 rhs_scale=lam_s[h, k][:],
-                start=(k == 0), stop=False,
+                start=(k == 0 and not phi_first), stop=(k == LG - 1 and phi_first),
             )
 
-        def z_phi(h, u, t):
+        def z_phi(h, u, t, phi_first=False):
+            if phi_first:
+                z_ps[h, u, t] = bank()
             cols = slice(128 * t, 128 * (t + 1))
             nc.tensor.matmul_mx(
                 out=z_ps[h, u, t][:], lhsT=g_q[u][:, cols].bitcast(FP8X4), lhsT_scale=g_s[u][:, cols],
-                rhs=phi_q[h][:].bitcast(FP8X4), rhs_scale=phi_s[h][:], start=False, stop=True,
+                rhs=phi_q[h][:].bitcast(FP8X4), rhs_scale=phi_s[h][:], start=phi_first, stop=not phi_first,
             )
 
         def exp(h, u, t):
@@ -299,8 +304,8 @@ def tile_equilibrium_mass_balance_s3_kernel(
         nc.vector.memset(one[:], 1.0)
 
         load_lam(0, 0)
-        nc.sync.dma_start(out=l_sc[:], in_=lam_scale.rearrange("o (k p t) -> p (o k) t", p=P, t=4))
         load_f(0)
+        nc.sync.dma_start(out=l_sc[:], in_=lam_scale.rearrange("o (k p t) -> p (o k) t", p=P, t=4))
         load_lam(0, 1)
         load_scales(f_first, f_scales[:, :, : 512 * FIRST])
         load_phi(0)
@@ -328,6 +333,7 @@ def tile_equilibrium_mass_balance_s3_kernel(
         lam_cast(0, 1, 1, "s")
         lam_turn(0, 1, 0)
         f_move(0)
+        f_scale(0, [0], "g")
         lam_cast(0, 0, 2, "s")
         lam_cast(0, 0, 3, "s")
         lam_mult(0, 0, 0)
@@ -340,7 +346,7 @@ def tile_equilibrium_mass_balance_s3_kernel(
         phi_turn(0, 1)
         lam_turn(0, 1, 1)
         warm_up(3)
-        f_scale(0)
+        f_scale(0, [1])
         lam_quant(0, 0)
         phi_copy(0, 0)
         phi_copy(0, 1)
@@ -376,9 +382,9 @@ def tile_equilibrium_mass_balance_s3_kernel(
             exp(0, 1, t)
         z_lams(0, 2, 0)
         z_lams(0, 2, 1)
-        f_scale(3)
         g_lay(3, 0, "v")
         g_lay(3, 1, "v")
+        f_scale(3)
         for t in FOUR:
             z_phi(0, 2, t)
             exp(0, 2, t)
@@ -397,16 +403,18 @@ def tile_equilibrium_mass_balance_s3_kernel(
             z_tile(0, 3, t)
             n_scale(0, 0, t)
         lam_mult(1, 1, 0)
-        lam_quant(1, 0)
-        lam_mult(1, 1, 1)
         phi_quant(1)
+        lam_mult(1, 1, 1)
+        lam_quant(1, 0)
         lam_quant(1, 1)
         n_mult(0, 2)
         n_lay(0, 0)
-        z_lams(1, 0, 0)
-        z_lams(1, 0, 1)
         for t in FOUR:
-            z_phi(1, 0, t)
+            z_phi(1, 0, t, True)
+        for t in FOUR:
+            z_lam(1, 0, t, 0, True)
+        for t in FOUR:
+            z_lam(1, 0, t, 1, True)
             n_scale(0, 1, t)
             exp(1, 0, t)
         n_quant(0, 2)

@@ -24,7 +24,11 @@ ROWS = 4
 UNITS = S // 512
 LG = E // 512
 FIRST = 2
-PHB = 1
+SLOT = {("lam", 0, 0): 0, ("g", 0): 0, ("lam", 1, 0): 0, ("lam", 0, 1): 1, ("g", 1): 5, ("lam", 1, 1): 1,
+        ("phi", 0): 2, ("g", 2): 2, ("phi", 1): 3, ("g", 3): 4}
+X, Y = (6, 7, 0, 1), (3, 2, 5, 4)
+ZB = {(0, 0): X, (0, 1): Y, (0, 2): X[2:] + Y[:2], (0, 3): Y[2:] + X[:2], (1, 0): Y, (1, 1): X, (1, 2): Y, (1, 3): X}
+OB = Y + X
 
 
 def tile_equilibrium_mass_balance_s3_kernel(
@@ -37,22 +41,24 @@ def tile_equilibrium_mass_balance_s3_kernel(
         psum = ctx.enter_context(tc.psum_pool(name="psum", bufs=1))
         ctx.enter_context(tc.manual_schedule())
 
-        lam_v = lam_bytes.rearrange("(h p a b) k -> h a p (b k)", h=2, a=2, b=2)
+        lam_v = lam_bytes.rearrange("(h p c) k -> h p c k", h=2, c=ROWS)
         phi_v = phi.rearrange("(h p c) k -> h p c k", h=2, c=ROWS)
         feed_v = feed.rearrange("(h p c) e -> h p c e", h=2, c=ROWS)
         out_v = out.rearrange("(h p c) e -> h p c e", h=2, c=ROWS)
         g_v = g.rearrange("(p j) s -> p j s", j=4)
-        f_v = f_words.rearrange("k p b -> p k b")
         a_v = a_words.rearrange("k p b -> p k b")
 
-        def bank():
-            return psum.tile([P, 512], F32, name="bank", tag="bank", bufs=8)
+        def bank(i):
+            return psum.tile([P, 512], F32, name="bank%d" % i)
+
+        def lay(*key):
+            return keep.tile([P, 512, 4], BF16, name="lay%d" % SLOT[key], align_bytes=64)
 
         lam_sb, phi_sb, feed_sb, g_sb, f_sb, f_raw = {}, {}, {}, {}, {}, {}
 
-        def load_lam(h, pair):
-            lam_sb[h, pair] = keep.tile([P, 2 * E], U8, name="lam_sb%d%d" % (h, pair))
-            nc.sync.dma_start(out=lam_sb[h, pair][:], in_=lam_v[h, pair])
+        def load_lam(h, k):
+            lam_sb[h, k] = keep.tile([P, ROWS, 512], U8, name="lam_sb%d%d" % (h, k))
+            nc.sync.dma_start(out=lam_sb[h, k][:], in_=lam_v[h][:, :, 512 * k : 512 * (k + 1)])
 
         def load_phi(h):
             phi_sb[h] = keep.tile([P, ROWS * D], BF16, name="phi_sb%d" % h)
@@ -66,9 +72,9 @@ def tile_equilibrium_mass_balance_s3_kernel(
             g_sb[u] = keep.tile([P, 4, 512], BF16, name="g_sb%d" % u)
             nc.sync.dma_start(out=g_sb[u][:], in_=g_v[:, :, 512 * u : 512 * (u + 1)])
 
-        def load_f(u):
-            f_sb[u] = keep.tile([P, LG, 1024], U8, name="f_sb%d" % u)
-            nc.sync.dma_start(out=f_sb[u][:], in_=f_v[:, :, 1024 * u : 1024 * (u + 1)])
+        def load_f(k, pair):
+            f_sb[k, pair] = keep.tile([P, 2048], U8, name="f_sb%d%d" % (k, pair))
+            nc.sync.dma_start(out=f_sb[k, pair][:], in_=f_words[k][:, 2048 * pair : 2048 * (pair + 1)])
 
         def scale_tile(name, passes, width):
             tile = keep.tile([P, passes, width], U8, name=name, align_bytes=64)
@@ -86,12 +92,11 @@ def tile_equilibrium_mass_balance_s3_kernel(
         def lam_cast(h, k, c, eng):
             if (h, k) not in wide:
                 wide[h, k] = work.tile([P, ROWS * 512], BF16, name="wide", tag="wide", bufs=2)
-            at = E * (c % 2) + 512 * k
             copy = nc.scalar.copy if eng == "s" else nc.vector.tensor_copy
-            copy(wide[h, k][:, 512 * c : 512 * (c + 1)], lam_sb[h, c // 2][:, at : at + 512].bitcast(FP8))
+            copy(wide[h, k][:, 512 * c : 512 * (c + 1)], lam_sb[h, k][:, c, :].bitcast(FP8))
 
-        def turn(key, rows, pair):
-            turned[key] = bank()
+        def turn(key, rows, pair, b):
+            turned[key] = bank(b)
             words = rows.bitcast(F32)
             for i in range(2):
                 c = 2 * pair + i
@@ -101,36 +106,38 @@ def tile_equilibrium_mass_balance_s3_kernel(
                         turned[key][:, at : at + 128], words[:, 256 * c + u : 256 * (c + 1) : 2], ident[:]
                     )
 
-        def lam_spread(h, pair):
-            wide[h, "p", pair] = work.tile([P, 2 * E], BF16, name="wide", tag="wide", bufs=2)
+        def lam_spread(h, k):
+            wide[h, k] = work.tile([P, ROWS * 512], BF16, name="wide", tag="wide", bufs=2)
             nc.vector.tensor_scalar(
-                out=wide[h, "p", pair][:].rearrange("p (u w e) -> p w u e", u=2, e=2),
-                in0=lam_sb[h, pair][:].bitcast(FP8).rearrange("p (w u e) -> p w u e", u=2, e=2),
+                out=wide[h, k][:].rearrange("p (u w e) -> p w u e", u=2, e=2),
+                in0=lam_sb[h, k][:].rearrange("p c k -> p (c k)").bitcast(FP8).rearrange("p (w u e) -> p w u e", u=2, e=2),
                 scalar1=one[:], scalar2=None, op0=ALU.mult,
             )
 
-        def lam_turn_whole(h, k, pair):
-            turned[h, k, pair] = bank()
-            words = wide[h, "p", pair][:].bitcast(F32)
+        def lam_turn_whole(h, k, pair, b):
+            turned[h, k, pair] = bank(b)
+            words = wide[h, k][:].bitcast(F32)
             for i in range(2):
                 for u in range(2):
-                    at, src = 256 * u + 128 * i, 512 * u + 256 * i + 128 * k
+                    at, src = 256 * u + 128 * i, 512 * u + 128 * (2 * pair + i)
                     nc.tensor.transpose(turned[h, k, pair][:, at : at + 128], words[:, src : src + 128], ident[:])
 
-        def warm_up(n):
-            wp = bank()
-            for i in range(n):
-                nc.tensor.matmul(wp[:], lhsT=phi_sb[0][:, 0:P], rhs=phi_sb[0][:, 0:512], start=True, stop=True)
+        def warm_up(blocks, b):
+            idle = bank(b)
+            nc.tensor.matmul(
+                idle[:, : P * blocks].rearrange("p (b n) -> p b n", n=P), lhsT=ident[:],
+                rhs=ident[:].unsqueeze(1).to_broadcast([P, blocks, P]), start=True, stop=True,
+            )
 
-        def lam_turn(h, k, pair):
-            turn((h, k, pair), wide[h, k][:], pair)
+        def lam_turn(h, k, pair, b):
+            turn((h, k, pair), wide[h, k][:], pair, b)
 
-        def phi_turn(h, pair):
-            turn((h, "phi", pair), phi_sb[h][:], pair)
+        def phi_turn(h, pair, b):
+            turn((h, "phi", pair), phi_sb[h][:], pair, b)
 
         def lam_mult(h, k, pair):
             if pair == 0:
-                lam_t[h, k] = work.tile([P, HALF, 4], BF16, name="lam_t", tag="lam_t", bufs=2, align_bytes=64)
+                lam_t[h, k] = lay("lam", h, k)
             nc.vector.tensor_tensor(
                 out=lam_t[h, k][:, 256 * pair : 256 * (pair + 1), :].rearrange("p r (u e) -> p r u e", e=2),
                 in0=turned[h, k, pair][:].bitcast(BF16).rearrange("p (u r e) -> p r u e", u=2, e=2),
@@ -140,7 +147,7 @@ def tile_equilibrium_mass_balance_s3_kernel(
 
         def phi_copy(h, pair):
             if pair == 0:
-                phi_t[h] = work.tile([P, HALF, 4], BF16, name="phi_t", tag="phi_t", bufs=PHB, align_bytes=64)
+                phi_t[h] = lay("phi", h)
             dst = phi_t[h][:].rearrange("p r t -> p (r t)").bitcast(F32).rearrange("p (r u) -> p r u", u=2)
             nc.scalar.copy(
                 dst[:, 256 * pair : 256 * (pair + 1)], turned[h, "phi", pair][:].rearrange("p (u r) -> p r u", u=2)
@@ -162,7 +169,7 @@ def tile_equilibrium_mass_balance_s3_kernel(
 
         def g_lay(u, i, eng):
             if u not in g_i:
-                g_i[u] = work.tile([P, 512, 4], BF16, name="gi", tag="gi", bufs=2, align_bytes=64)
+                g_i[u] = lay("g", u)
             ms = slice(32 * i, 32 * i + 32)
             copy = nc.scalar.copy if eng == "s" else nc.vector.tensor_copy
             copy(
@@ -170,34 +177,47 @@ def tile_equilibrium_mass_balance_s3_kernel(
                 g_sb[u][:].rearrange("p j (a b t) -> p a j b t", t=4, b=2)[:, ms],
             )
 
+        def g_lay_t(u, i, eng):
+            if u not in g_i:
+                g_i[u] = lay("g", u)
+            ts = slice(2 * i, 2 * i + 2)
+            dst = g_i[u][:].rearrange("p (t m) j -> p t m j", t=4)[:, ts]
+            src = g_sb[u][:].rearrange("p j (m t) -> p t m j", t=4)[:, ts]
+            if eng == "g":
+                nc.gpsimd.tensor_scalar(out=dst, in0=src, scalar1=1.0, scalar2=0.0, op0=ALU.mult, op1=ALU.add)
+            else:
+                nc.scalar.copy(dst, src)
+
         def g_quant(u):
             g_q[u], g_s[u] = quantise("g%d" % u, g_i[u])
 
-        def f_move(u, eng="v"):
-            f_p[u] = keep.tile([P, LG, 1024], U8, name="f_p%d" % u, align_bytes=64)
-            (nc.gpsimd if eng == "g" else nc.vector).tensor_copy(
-                out=f_p[u][:].bitcast(U16).rearrange("p k (t m) -> p k t m", t=4),
-                in_=f_sb[u][:].bitcast(U16).rearrange("p k (m t) -> p k t m", t=4),
+        def f_move(k, first, count=1):
+            pair, at = divmod(first, 2)
+            if (k, pair) not in f_p:
+                f_p[k, pair] = keep.tile([P, 2, 1024], U8, name="f_p%d%d" % (k, pair), align_bytes=64)
+            nc.vector.tensor_copy(
+                out=f_p[k, pair][:, at : at + count].bitcast(U16).rearrange("p u (t m) -> p u t m", t=4),
+                in_=f_sb[k, pair][:].bitcast(U16).rearrange("p (u m t) -> p u t m", u=2, t=4)[:, at : at + count],
             )
 
-        def f_scale(u, ks=range(LG), eng="v"):
-            if u not in f_sp:
-                f_sp[u] = keep.tile([P, LG, 512], U8, name="f_sp%d" % u, align_bytes=64)
-            ks = slice(ks[0], ks[-1] + 1)
+        def f_scale(k, first, count=1, eng="v"):
+            pair, at = divmod(first, 2)
+            if (k, pair) not in f_sp:
+                f_sp[k, pair] = keep.tile([P, 2, 512], U8, name="f_sp%d%d" % (k, pair), align_bytes=64)
             (nc.gpsimd if eng == "g" else nc.vector).tensor_copy(
-                out=f_sp[u][:, ks].rearrange("p k (t m) -> p k t m", t=4),
-                in_=f_raw[u][:, ks].rearrange("p k (m t) -> p k t m", t=4),
+                out=f_sp[k, pair][:, at : at + count].rearrange("p u (t m) -> p u t m", t=4),
+                in_=f_raw[pair][:, k].rearrange("p (u m t) -> p u t m", u=2, t=4)[:, at : at + count],
             )
 
         e_sb, flat, nb, n_q, n_s, z_ps = {}, {}, {}, {}, {}, {}
 
         def z_lam(h, u, t, k, phi_first=False):
             if k == 0 and not phi_first:
-                z_ps[h, u, t] = bank()
+                z_ps[h, u, t] = bank(ZB[h, u][t])
             nc.tensor.matmul_mx(
                 out=z_ps[h, u, t][:],
-                lhsT=f_p[u][:, k, 256 * t : 256 * (t + 1)].bitcast(FP4X4),
-                lhsT_scale=f_sp[u][:, k, 128 * t : 128 * (t + 1)],
+                lhsT=f_p[k, u // 2][:, u % 2, 256 * t : 256 * (t + 1)].bitcast(FP4X4),
+                lhsT_scale=f_sp[k, u // 2][:, u % 2, 128 * t : 128 * (t + 1)],
                 rhs=lam_q[h, k][:].bitcast(FP8X4),
                 rhs_scale=lam_s[h, k][:],
                 start=(k == 0 and not phi_first), stop=(k == LG - 1 and phi_first),
@@ -205,7 +225,7 @@ def tile_equilibrium_mass_balance_s3_kernel(
 
         def z_phi(h, u, t, phi_first=False):
             if phi_first:
-                z_ps[h, u, t] = bank()
+                z_ps[h, u, t] = bank(ZB[h, u][t])
             cols = slice(128 * t, 128 * (t + 1))
             nc.tensor.matmul_mx(
                 out=z_ps[h, u, t][:], lhsT=g_q[u][:, cols].bitcast(FP8X4), lhsT_scale=g_s[u][:, cols],
@@ -219,7 +239,7 @@ def tile_equilibrium_mass_balance_s3_kernel(
 
         def n_scale(h, u, t):
             if t == 0:
-                flat[h, u] = work.tile([P, 4, HALF], BF16, name="flat", tag="flat", bufs=2)
+                flat[h, u] = work.tile([P, 4, HALF], BF16, name="flat", tag="wide", bufs=2)
             nc.scalar.activation(
                 flat[h, u][:, t, :], e_sb[h, u][:, t, :], ACT.Copy, scale=m_f[:, 4 * u + t : 4 * u + t + 1]
             )
@@ -231,12 +251,13 @@ def tile_equilibrium_mass_balance_s3_kernel(
                 in_=flat[h, u][:].rearrange("p t (r i) -> p r t i", i=4),
             )
 
-        def n_mult(h, u):
-            nb[h, u] = work.tile([P, HALF, 4], BF16, name="nb", tag="nb", bufs=2, align_bytes=64)
+        def n_mult(h, u, first=0, last=HALF // 4):
+            if first == 0:
+                nb[h, u] = work.tile([P, HALF, 4], BF16, name="nb", tag="nb", bufs=2, align_bytes=64)
             nc.vector.tensor_tensor(
-                out=nb[h, u][:].rearrange("p (r i) t -> p r t i", i=4),
-                in0=e_sb[h, u][:].rearrange("p t (r i) -> p r t i", i=4),
-                in1=m_f[:, 4 * u : 4 * u + 4].unsqueeze(1).unsqueeze(3).to_broadcast([P, HALF // 4, 4, 4]),
+                out=nb[h, u][:].rearrange("p (r i) t -> p r t i", i=4)[:, first:last],
+                in0=e_sb[h, u][:].rearrange("p t (r i) -> p r t i", i=4)[:, first:last],
+                in1=m_f[:, 4 * u : 4 * u + 4].unsqueeze(1).unsqueeze(3).to_broadcast([P, last - first, 4, 4]),
                 op=ALU.mult,
             )
 
@@ -246,7 +267,7 @@ def tile_equilibrium_mass_balance_s3_kernel(
         acc = {}
 
         def balance(h, c, e):
-            acc[h, c, e] = bank()
+            acc[h, c, e] = bank(OB[2 * c + e])
             cols = slice(128 * c, 128 * (c + 1))
             for u in range(UNITS):
                 nc.tensor.matmul_mx(
@@ -269,8 +290,8 @@ def tile_equilibrium_mass_balance_s3_kernel(
 
         FOUR = range(4)
 
-        def z_lams(h, u, k):
-            for t in FOUR:
+        def z_lams(h, u, k, tiles=FOUR):
+            for t in tiles:
                 z_lam(h, u, t, k)
 
         def z_tile(h, u, t):
@@ -292,9 +313,7 @@ def tile_equilibrium_mass_balance_s3_kernel(
         ident = keep.tile([P, P], F32, name="ident")
         make_identity(nc, ident[:])
         f_rest = scale_tile("f_rest", LG, S - 512 * FIRST)
-        for u in range(UNITS):
-            src, at = (f_first, u) if u < FIRST else (f_rest, u - FIRST)
-            f_raw[u] = src[:, :, 512 * at : 512 * (at + 1)]
+        f_raw[0], f_raw[1] = f_first, f_rest
         a_sc = scale_tile("a_sc", UNITS, E)
         l_sc = keep.tile([P, LG, 4], F32, name="l_sc")
         m_sb = keep.tile([P, UNITS, 4], BF16, name="m_sb")
@@ -304,127 +323,148 @@ def tile_equilibrium_mass_balance_s3_kernel(
         nc.vector.memset(one[:], 1.0)
 
         load_lam(0, 0)
-        load_f(0)
+        load_f(0, 0)
         nc.sync.dma_start(out=l_sc[:], in_=lam_scale.rearrange("o (k p t) -> p (o k) t", p=P, t=4))
         load_lam(0, 1)
         load_scales(f_first, f_scales[:, :, : 512 * FIRST])
         load_phi(0)
         load_g(0)
-        load_f(1)
-        load_g(1)
-        load_scales(f_rest, f_scales[:, :, 512 * FIRST :])
-        load_f(2)
-        load_g(2)
-        load_lam(1, 0)
-        load_lam(1, 1)
-        load_f(3)
-        load_g(3)
-        nc.sync.dma_start(out=m_sb[:], in_=m.rearrange("(u p t) -> p u t", p=P, t=4))
+        load_f(1, 0)
         load_phi(1)
+        load_g(1)
+        load_lam(1, 0)
+        load_scales(f_rest, f_scales[:, :, 512 * FIRST :])
+        load_f(0, 1)
+        load_g(2)
+        load_f(1, 1)
+        load_g(3)
+        load_lam(1, 1)
+        nc.sync.dma_start(out=m_sb[:], in_=m.rearrange("(u p t) -> p u t", p=P, t=4))
         load_scales(a_sc, a_scales)
         nc.sync.dma_start(out=a_sb[:], in_=a_v)
         load_feed(0)
         load_feed(1)
 
+        warm_up(3, 6)
         lam_cast(0, 0, 0, "v")
-        lam_cast(0, 0, 1, "s")
-        lam_turn(0, 0, 0)
-        lam_cast(0, 1, 0, "s")
-        lam_cast(0, 1, 1, "s")
-        lam_turn(0, 1, 0)
-        f_move(0)
-        f_scale(0, [0], "g")
+        lam_cast(0, 0, 1, "v")
         lam_cast(0, 0, 2, "s")
         lam_cast(0, 0, 3, "s")
+        lam_turn(0, 0, 0, 0)
+        lam_turn(0, 0, 1, 1)
+        warm_up(2, 6)
+        f_move(0, 0, 2)
+        f_scale(0, 0, 1, "g")
+        for c in FOUR:
+            lam_cast(0, 1, c, "s")
         lam_mult(0, 0, 0)
-        lam_turn(0, 0, 1)
-        lam_cast(0, 1, 2, "s")
-        lam_cast(0, 1, 3, "s")
-        lam_mult(0, 1, 0)
         lam_mult(0, 0, 1)
-        phi_turn(0, 0)
-        phi_turn(0, 1)
-        lam_turn(0, 1, 1)
-        warm_up(3)
-        f_scale(0, [1])
+        f_scale(0, 1)
+        lam_turn(0, 1, 0, 2)
+        warm_up(1, 6)
+        phi_turn(0, 0, 3)
+        lam_turn(0, 1, 1, 4)
+        phi_turn(0, 1, 5)
         lam_quant(0, 0)
         phi_copy(0, 0)
         phi_copy(0, 1)
-        z_lams(0, 0, 0)
+        g_lay_t(0, 0, "s")
+        g_lay_t(0, 1, "g")
+        lam_mult(0, 1, 0)
         lam_mult(0, 1, 1)
-        g_lay(0, 0, "s")
-        g_lay(0, 1, "s")
-        phi_quant(0)
+        z_lams(0, 0, 0)
+        z_lams(0, 1, 0, (0, 1))
+        phi_turn(1, 0, 5)
+        phi_turn(1, 1, 4)
+        f_move(1, 0)
+        f_scale(1, 0)
         lam_quant(0, 1)
+        phi_quant(0)
         g_quant(0)
         z_lams(0, 0, 1)
         g_lay(1, 0, "s")
         g_lay(1, 1, "s")
-        f_move(1)
-        f_scale(1)
+        phi_copy(1, 0)
+        phi_copy(1, 1)
+        f_move(1, 1)
+        f_scale(1, 1)
         for t in FOUR:
             z_phi(0, 0, t)
             exp(0, 0, t)
-        z_lams(0, 1, 0)
-        z_lams(0, 1, 1)
-        f_move(2)
+        z_lams(0, 1, 1, (0, 1))
+        f_move(0, 2, 1)
+        f_scale(0, 2, 1)
         g_quant(1)
-        f_scale(2)
-        for t in FOUR:
-            z_phi(0, 1, t)
-        g_lay(2, 0, "s")
-        g_lay(2, 1, "s")
         lam_spread(1, 0)
-        lam_spread(1, 1)
-        f_move(3)
-        g_quant(2)
+        z_phi(0, 1, 0)
+        z_phi(0, 1, 1)
+        for t in (2, 3):
+            for k in range(LG):
+                z_lam(0, 1, t, k)
+            z_phi(0, 1, t)
+        lam_turn_whole(1, 0, 0, X[0])
+        lam_turn_whole(1, 0, 1, X[1])
+        g_lay(2, 0, "s")
+        f_move(1, 2, 1)
+        f_scale(1, 2, 1)
+        f_move(0, 3, 1)
+        f_scale(0, 3, 1)
+        g_lay(2, 1, "v")
         for t in FOUR:
             exp(0, 1, t)
-        z_lams(0, 2, 0)
-        z_lams(0, 2, 1)
-        g_lay(3, 0, "v")
-        g_lay(3, 1, "v")
-        f_scale(3)
+        lam_mult(1, 0, 0)
+        g_quant(2)
+        lam_mult(1, 0, 1)
+        for t in FOUR:
+            for k in range(LG):
+                z_lam(0, 2, t, k)
+        g_lay(3, 0, "s")
         for t in FOUR:
             z_phi(0, 2, t)
             exp(0, 2, t)
+        f_move(1, 3, 1)
+        f_scale(1, 3, 1)
+        g_lay(3, 1, "v")
         nc.vector.tensor_copy(out=m_f[:], in_=m_sb[:].rearrange("p u t -> p (u t)"))
-        g_quant(3)
-        for k in range(LG):
-            lam_turn_whole(1, k, 0)
-            lam_turn_whole(1, k, 1)
-        phi_turn(1, 0)
-        phi_turn(1, 1)
-        lam_mult(1, 0, 0)
-        lam_mult(1, 0, 1)
-        phi_copy(1, 0)
-        phi_copy(1, 1)
-        for t in FOUR:
-            z_tile(0, 3, t)
-            n_scale(0, 0, t)
-        lam_mult(1, 1, 0)
         phi_quant(1)
-        lam_mult(1, 1, 1)
+        g_quant(3)
+        lam_spread(1, 1)
         lam_quant(1, 0)
+        for t in FOUR:
+            for k in range(LG):
+                z_lam(0, 3, t, k)
+        for t in FOUR:
+            z_phi(0, 3, t)
+        for t in FOUR:
+            n_scale(0, 0, t)
+            exp(0, 3, t)
+        lam_turn_whole(1, 1, 0, X[2])
+        lam_turn_whole(1, 1, 1, X[3])
+        n_mult(0, 2, 0, 64)
+        lam_mult(1, 1, 0)
+        lam_mult(1, 1, 1)
+        for h, u, t in ((1, 0, 0), (1, 0, 1), (1, 0, 2), (1, 0, 3), (1, 1, 0), (1, 1, 1)):
+            z_phi(h, u, t, True)
+            z_lam(h, u, t, 0, True)
+        scale_unit(0, 1)
         lam_quant(1, 1)
-        n_mult(0, 2)
+        n_mult(0, 2, 64, 128)
         n_lay(0, 0)
         for t in FOUR:
-            z_phi(1, 0, t, True)
-        for t in FOUR:
-            z_lam(1, 0, t, 0, True)
-        for t in FOUR:
             z_lam(1, 0, t, 1, True)
-            n_scale(0, 1, t)
             exp(1, 0, t)
+        for t in (0, 1):
+            z_lam(1, 1, t, 1, True)
+            exp(1, 1, t)
         n_quant(0, 2)
         n_mult(0, 3)
         n_quant(0, 0)
-        z_unit(1, 1)
+        z_tile(1, 1, 2)
+        z_tile(1, 1, 3)
         n_lay(0, 1)
         n_quant(0, 3)
-        n_mult(1, 0)
         n_quant(0, 1)
+        n_mult(1, 0)
         for t in FOUR:
             z_tile(1, 2, t)
             n_scale(1, 1, t)

@@ -24,6 +24,7 @@ ROWS = 4
 UNITS = S // 512
 LG = E // 512
 FIRST = 2
+NB = 3
 SLOT = {("lam", 0, 0): 0, ("g", 0): 0, ("lam", 1, 0): 0, ("lam", 0, 1): 1, ("g", 1): 5, ("lam", 1, 1): 1,
         ("phi", 0): 2, ("g", 2): 2, ("phi", 1): 3, ("g", 3): 4}
 X, Y = (6, 7, 0, 1), (3, 2, 5, 4)
@@ -60,13 +61,13 @@ def tile_equilibrium_mass_balance_s3_kernel(
             lam_sb[h, k] = keep.tile([P, ROWS, 512], U8, name="lam_sb%d%d" % (h, k))
             nc.sync.dma_start(out=lam_sb[h, k][:], in_=lam_v[h][:, :, 512 * k : 512 * (k + 1)])
 
-        def load_phi(h):
-            phi_sb[h] = keep.tile([P, ROWS * D], BF16, name="phi_sb%d" % h)
-            nc.sync.dma_start(out=phi_sb[h][:], in_=phi_v[h].rearrange("p c k -> p (c k)"))
+        def load_phi(h, pair):
+            phi_sb[h, pair] = keep.tile([P, 2 * D], BF16, name="phi_sb%d%d" % (h, pair))
+            nc.sync.dma_start(out=phi_sb[h, pair][:], in_=phi_v[h][:, 2 * pair : 2 * pair + 2].rearrange("p c k -> p (c k)"))
 
-        def load_feed(h):
-            feed_sb[h] = keep.tile([P, ROWS, E], BF16, name="feed_sb%d" % h)
-            nc.sync.dma_start(out=feed_sb[h][:], in_=feed_v[h])
+        def load_feed(h, pair):
+            feed_sb[h, pair] = keep.tile([P, 2, E], BF16, name="g_sb%d" % (2 * h + pair))
+            nc.sync.dma_start(out=feed_sb[h, pair][:], in_=feed_v[h][:, 2 * pair : 2 * pair + 2])
 
         def load_g(u):
             g_sb[u] = keep.tile([P, 4, 512], BF16, name="g_sb%d" % u)
@@ -133,7 +134,7 @@ def tile_equilibrium_mass_balance_s3_kernel(
             turn((h, k, pair), wide[h, k][:], pair, b)
 
         def phi_turn(h, pair, b):
-            turn((h, "phi", pair), phi_sb[h][:], pair, b)
+            turn((h, "phi", pair), phi_sb[h, pair][:], 0, b)
 
         def lam_mult(h, k, pair):
             if pair == 0:
@@ -167,20 +168,20 @@ def tile_equilibrium_mass_balance_s3_kernel(
 
         g_q, g_s, f_p, f_sp, g_i = {}, {}, {}, {}, {}
 
-        def g_lay(u, i, eng):
+        def g_lay(u, first, last, eng, tiles=4):
             if u not in g_i:
                 g_i[u] = lay("g", u)
-            ms = slice(32 * i, 32 * i + 32)
+            ms = slice(8 * first, 8 * last)
             copy = nc.scalar.copy if eng == "s" else nc.vector.tensor_copy
             copy(
-                g_i[u][:].rearrange("p (t a b) j -> p a j b t", t=4, b=2)[:, ms],
-                g_sb[u][:].rearrange("p j (a b t) -> p a j b t", t=4, b=2)[:, ms],
+                g_i[u][:].rearrange("p (t a b) j -> p a j b t", t=4, b=2)[:, ms, :, :, :tiles],
+                g_sb[u][:].rearrange("p j (a b t) -> p a j b t", t=4, b=2)[:, ms, :, :, :tiles],
             )
 
         def g_lay_t(u, i, eng):
             if u not in g_i:
                 g_i[u] = lay("g", u)
-            ts = slice(2 * i, 2 * i + 2)
+            ts = slice(i[0], i[-1] + 1)
             dst = g_i[u][:].rearrange("p (t m) j -> p t m j", t=4)[:, ts]
             src = g_sb[u][:].rearrange("p j (m t) -> p t m j", t=4)[:, ts]
             if eng == "g":
@@ -200,13 +201,16 @@ def tile_equilibrium_mass_balance_s3_kernel(
                 in_=f_sb[k, pair][:].bitcast(U16).rearrange("p (u m t) -> p u t m", u=2, t=4)[:, at : at + count],
             )
 
-        def f_scale(k, first, count=1, eng="v"):
-            pair, at = divmod(first, 2)
-            if (k, pair) not in f_sp:
-                f_sp[k, pair] = keep.tile([P, 2, 512], U8, name="f_sp%d%d" % (k, pair), align_bytes=64)
+        def f_scale(u, ks, eng="v", slot=None):
+            if slot is None:
+                dst = keep.tile([P, len(ks), 512], U8, name="f_sp%d%d" % (u, ks[0]), align_bytes=64)[:]
+            else:
+                dst = lay(*slot)[:].rearrange("p r t -> p (r t)")[:, : 256 * len(ks)].bitcast(U8).rearrange("p (k n) -> p k n", n=512)
+            for i, k in enumerate(ks):
+                f_sp[u, k] = dst[:, i, :]
             (nc.gpsimd if eng == "g" else nc.vector).tensor_copy(
-                out=f_sp[k, pair][:, at : at + count].rearrange("p u (t m) -> p u t m", t=4),
-                in_=f_raw[pair][:, k].rearrange("p (u m t) -> p u t m", u=2, t=4)[:, at : at + count],
+                out=dst.rearrange("p k (t m) -> p k t m", t=4),
+                in_=f_raw[u // 2][:, ks[0] : ks[-1] + 1, 512 * (u % 2) : 512 * (u % 2 + 1)].rearrange("p k (m t) -> p k t m", t=4),
             )
 
         e_sb, flat, nb, n_q, n_s, z_ps = {}, {}, {}, {}, {}, {}
@@ -217,7 +221,7 @@ def tile_equilibrium_mass_balance_s3_kernel(
             nc.tensor.matmul_mx(
                 out=z_ps[h, u, t][:],
                 lhsT=f_p[k, u // 2][:, u % 2, 256 * t : 256 * (t + 1)].bitcast(FP4X4),
-                lhsT_scale=f_sp[k, u // 2][:, u % 2, 128 * t : 128 * (t + 1)],
+                lhsT_scale=f_sp[u, k][:, 128 * t : 128 * (t + 1)],
                 rhs=lam_q[h, k][:].bitcast(FP8X4),
                 rhs_scale=lam_s[h, k][:],
                 start=(k == 0 and not phi_first), stop=(k == LG - 1 and phi_first),
@@ -244,16 +248,16 @@ def tile_equilibrium_mass_balance_s3_kernel(
                 flat[h, u][:, t, :], e_sb[h, u][:, t, :], ACT.Copy, scale=m_f[:, 4 * u + t : 4 * u + t + 1]
             )
 
-        def n_lay(h, u):
-            nb[h, u] = work.tile([P, HALF, 4], BF16, name="nb", tag="nb", bufs=2, align_bytes=64)
-            nc.vector.tensor_copy(
-                out=nb[h, u][:].rearrange("p (r i) t -> p r t i", i=4),
-                in_=flat[h, u][:].rearrange("p t (r i) -> p r t i", i=4),
+        def n_lay(h, u, eng="v"):
+            nb[h, u] = work.tile([P, HALF, 4], BF16, name="nb", tag="nb", bufs=NB, align_bytes=64)
+            (nc.scalar.copy if eng == "s" else nc.vector.tensor_copy)(
+                nb[h, u][:].rearrange("p (r i) t -> p r t i", i=4),
+                flat[h, u][:].rearrange("p t (r i) -> p r t i", i=4),
             )
 
         def n_mult(h, u, first=0, last=HALF // 4):
             if first == 0:
-                nb[h, u] = work.tile([P, HALF, 4], BF16, name="nb", tag="nb", bufs=2, align_bytes=64)
+                nb[h, u] = work.tile([P, HALF, 4], BF16, name="nb", tag="nb", bufs=NB, align_bytes=64)
             nc.vector.tensor_tensor(
                 out=nb[h, u][:].rearrange("p (r i) t -> p r t i", i=4)[:, first:last],
                 in0=e_sb[h, u][:].rearrange("p t (r i) -> p r t i", i=4)[:, first:last],
@@ -278,13 +282,29 @@ def tile_equilibrium_mass_balance_s3_kernel(
                     start=(u == 0), stop=(u == UNITS - 1),
                 )
 
+        def last_columns(h, c, e, banks):
+            rows = slice(128 * c, 128 * (c + 1))
+            for i, b in enumerate(banks):
+                at = 512 * e + 128 * i
+                part = bank(b)
+                for u in range(UNITS):
+                    nc.tensor.matmul_mx(
+                        out=part[:, :P],
+                        lhsT=n_q[h, u][:, rows].bitcast(FP8X4), lhsT_scale=n_s[h, u][:, rows],
+                        rhs=a_sb[:, u, 2 * at : 2 * (at + P)].bitcast(FP4X4), rhs_scale=a_sc[:, u, at : at + P],
+                        start=(u == 0), stop=(u == UNITS - 1),
+                    )
+                o = work.tile([P, P], F32, name="o", tag="o", bufs=10)
+                nc.vector.tensor_tensor(out=o[:], in0=part[:, :P], in1=feed_sb[h, c // 2][:, c % 2, at : at + P], op=ALU.subtract)
+                nc.sync.dma_start(out=out_v[h][:, c, at : at + P], in_=o[:])
+
         def finish(h, c, e, parts=1):
             w = 512 // parts
             for i in range(parts):
                 cols = slice(512 * e + w * i, 512 * e + w * (i + 1))
-                o = work.tile([P, w], F32, name="o", tag="o", bufs=5)
+                o = work.tile([P, w], F32, name="o", tag="o", bufs=10)
                 nc.vector.tensor_tensor(
-                    out=o[:], in0=acc[h, c, e][:, w * i : w * (i + 1)], in1=feed_sb[h][:, c, cols], op=ALU.subtract
+                    out=o[:], in0=acc[h, c, e][:, w * i : w * (i + 1)], in1=feed_sb[h, c // 2][:, c % 2, cols], op=ALU.subtract
                 )
                 nc.sync.dma_start(out=out_v[h][:, c, cols], in_=o[:])
 
@@ -327,10 +347,12 @@ def tile_equilibrium_mass_balance_s3_kernel(
         nc.sync.dma_start(out=l_sc[:], in_=lam_scale.rearrange("o (k p t) -> p (o k) t", p=P, t=4))
         load_lam(0, 1)
         load_scales(f_first, f_scales[:, :, : 512 * FIRST])
-        load_phi(0)
+        load_phi(0, 0)
+        load_phi(0, 1)
         load_g(0)
         load_f(1, 0)
-        load_phi(1)
+        load_phi(1, 0)
+        load_phi(1, 1)
         load_g(1)
         load_lam(1, 0)
         load_scales(f_rest, f_scales[:, :, 512 * FIRST :])
@@ -342,8 +364,6 @@ def tile_equilibrium_mass_balance_s3_kernel(
         nc.sync.dma_start(out=m_sb[:], in_=m.rearrange("(u p t) -> p u t", p=P, t=4))
         load_scales(a_sc, a_scales)
         nc.sync.dma_start(out=a_sb[:], in_=a_v)
-        load_feed(0)
-        load_feed(1)
 
         warm_up(3, 6)
         lam_cast(0, 0, 0, "v")
@@ -354,12 +374,12 @@ def tile_equilibrium_mass_balance_s3_kernel(
         lam_turn(0, 0, 1, 1)
         warm_up(2, 6)
         f_move(0, 0, 2)
-        f_scale(0, 0, 1, "g")
+        f_scale(0, (0,), "g")
         for c in FOUR:
             lam_cast(0, 1, c, "s")
         lam_mult(0, 0, 0)
         lam_mult(0, 0, 1)
-        f_scale(0, 1)
+        f_scale(1, (0,))
         lam_turn(0, 1, 0, 2)
         warm_up(1, 6)
         phi_turn(0, 0, 3)
@@ -367,9 +387,11 @@ def tile_equilibrium_mass_balance_s3_kernel(
         phi_turn(0, 1, 5)
         lam_quant(0, 0)
         phi_copy(0, 0)
+        g_lay(0, 0, 4, "s", 3)
         phi_copy(0, 1)
-        g_lay_t(0, 0, "s")
-        g_lay_t(0, 1, "g")
+        g_lay(0, 4, 8, "s", 3)
+        g_lay_t(0, (3,), "g")
+        f_scale(0, (1,), "g")
         lam_mult(0, 1, 0)
         lam_mult(0, 1, 1)
         z_lams(0, 0, 0)
@@ -377,70 +399,69 @@ def tile_equilibrium_mass_balance_s3_kernel(
         phi_turn(1, 0, 5)
         phi_turn(1, 1, 4)
         f_move(1, 0)
-        f_scale(1, 0)
         lam_quant(0, 1)
         phi_quant(0)
         g_quant(0)
         z_lams(0, 0, 1)
-        g_lay(1, 0, "s")
-        g_lay(1, 1, "s")
+        g_lay(1, 0, 4, "s")
         phi_copy(1, 0)
         phi_copy(1, 1)
+        g_lay(1, 4, 6, "s")
         f_move(1, 1)
-        f_scale(1, 1)
+        f_scale(1, (1,))
         for t in FOUR:
             z_phi(0, 0, t)
             exp(0, 0, t)
         z_lams(0, 1, 1, (0, 1))
-        f_move(0, 2, 1)
-        f_scale(0, 2, 1)
-        g_quant(1)
-        lam_spread(1, 0)
-        z_phi(0, 1, 0)
-        z_phi(0, 1, 1)
         for t in (2, 3):
             for k in range(LG):
                 z_lam(0, 1, t, k)
+        g_lay(1, 6, 8, "v")
+        lam_spread(1, 0)
+        g_quant(1)
+        f_move(0, 2, 2)
+        for t in FOUR:
             z_phi(0, 1, t)
         lam_turn_whole(1, 0, 0, X[0])
         lam_turn_whole(1, 0, 1, X[1])
-        g_lay(2, 0, "s")
-        f_move(1, 2, 1)
-        f_scale(1, 2, 1)
-        f_move(0, 3, 1)
-        f_scale(0, 3, 1)
-        g_lay(2, 1, "v")
+        g_lay(2, 0, 4, "s")
+        f_scale(2, (0, 1))
+        f_move(1, 2, 2)
+        g_lay(2, 4, 8, "v")
         for t in FOUR:
             exp(0, 1, t)
-        lam_mult(1, 0, 0)
+        f_scale(3, (1,))
         g_quant(2)
+        f_scale(3, (0,), "g", ("g", 2))
+        lam_mult(1, 0, 0)
         lam_mult(1, 0, 1)
         for t in FOUR:
             for k in range(LG):
                 z_lam(0, 2, t, k)
-        g_lay(3, 0, "s")
+        g_lay(3, 0, 5, "s")
         for t in FOUR:
             z_phi(0, 2, t)
             exp(0, 2, t)
-        f_move(1, 3, 1)
-        f_scale(1, 3, 1)
-        g_lay(3, 1, "v")
+        g_lay(3, 5, 8, "v")
+        for i in FOUR:
+            load_feed(i // 2, i % 2)
         nc.vector.tensor_copy(out=m_f[:], in_=m_sb[:].rearrange("p u t -> p (u t)"))
-        phi_quant(1)
         g_quant(3)
         lam_spread(1, 1)
+        phi_quant(1)
         lam_quant(1, 0)
         for t in FOUR:
             for k in range(LG):
                 z_lam(0, 3, t, k)
         for t in FOUR:
             z_phi(0, 3, t)
+        exp(0, 3, 0)
         for t in FOUR:
+            if t < 3:
+                exp(0, 3, t + 1)
             n_scale(0, 0, t)
-            exp(0, 3, t)
         lam_turn_whole(1, 1, 0, X[2])
         lam_turn_whole(1, 1, 1, X[3])
-        n_mult(0, 2, 0, 64)
         lam_mult(1, 1, 0)
         lam_mult(1, 1, 1)
         for h, u, t in ((1, 0, 0), (1, 0, 1), (1, 0, 2), (1, 0, 3), (1, 1, 0), (1, 1, 1)):
@@ -448,7 +469,7 @@ def tile_equilibrium_mass_balance_s3_kernel(
             z_lam(h, u, t, 0, True)
         scale_unit(0, 1)
         lam_quant(1, 1)
-        n_mult(0, 2, 64, 128)
+        n_mult(0, 2)
         n_lay(0, 0)
         for t in FOUR:
             z_lam(1, 0, t, 1, True)
@@ -465,24 +486,25 @@ def tile_equilibrium_mass_balance_s3_kernel(
         n_quant(0, 3)
         n_quant(0, 1)
         n_mult(1, 0)
-        for t in FOUR:
-            z_tile(1, 2, t)
-            n_scale(1, 1, t)
-        z_unit(1, 3)
-        scale_unit(1, 2)
-        n_lay(1, 1)
+        z_unit(1, 2)
+        n_mult(1, 1)
         n_quant(1, 0)
+        for t in FOUR:
+            n_scale(1, 2, t)
+            z_tile(1, 3, t)
+        n_lay(1, 2, "s")
+        n_quant(1, 1)
         for c in FOUR:
             for e in range(2):
                 balance(0, c, e)
         finish(0, 0, 0)
-        n_quant(1, 1)
         n_mult(1, 3)
-        n_lay(1, 2)
-        n_quant(1, 3)
         finish(0, 0, 1)
+        n_quant(1, 3)
+        finish(0, 1, 0)
         n_quant(1, 2)
-        for c in (1, 2, 3):
+        finish(0, 1, 1)
+        for c in (2, 3):
             for e in range(2):
                 finish(0, c, e)
         for c in FOUR:

@@ -273,13 +273,13 @@ def tile_equilibrium_mass_balance_s3_kernel(
         def balance(h, c, e):
             acc[h, c, e] = bank(OB[2 * c + e])
             cols = slice(128 * c, 128 * (c + 1))
-            for u in range(UNITS):
+            for u in (0, 1, 3, 2):
                 nc.tensor.matmul_mx(
                     out=acc[h, c, e][:],
                     lhsT=n_q[h, u][:, cols].bitcast(FP8X4), lhsT_scale=n_s[h, u][:, cols],
                     rhs=a_sb[:, u, 1024 * e : 1024 * (e + 1)].bitcast(FP4X4),
                     rhs_scale=a_sc[:, u, 512 * e : 512 * (e + 1)],
-                    start=(u == 0), stop=(u == UNITS - 1),
+                    start=(u == 0), stop=(u == 2),
                 )
 
         def last_columns(h, c, e, banks):
@@ -486,27 +486,26 @@ def tile_equilibrium_mass_balance_s3_kernel(
         n_quant(0, 3)
         n_quant(0, 1)
         n_mult(1, 0)
-        z_unit(1, 2)
-        n_mult(1, 1)
-        n_quant(1, 0)
         for t in FOUR:
-            n_scale(1, 2, t)
-            z_tile(1, 3, t)
-        n_lay(1, 2, "s")
-        n_quant(1, 1)
+            z_tile(1, 2, t)
+            n_scale(1, 1, t)
+        z_unit(1, 3)
+        scale_unit(1, 2)
+        n_lay(1, 1)
+        n_quant(1, 0)
         for c in FOUR:
             for e in range(2):
                 balance(0, c, e)
-        finish(0, 0, 0)
+        n_quant(1, 1)
         n_mult(1, 3)
-        finish(0, 0, 1)
+        n_lay(1, 2)
         n_quant(1, 3)
-        finish(0, 1, 0)
+        finish(0, 0, 0)
         n_quant(1, 2)
-        finish(0, 1, 1)
-        for c in (2, 3):
+        for c in FOUR:
             for e in range(2):
-                finish(0, c, e)
+                if (c, e) != (0, 0):
+                    finish(0, c, e)
         for c in FOUR:
             for e in range(2):
                 balance(1, c, e)

@@ -168,26 +168,25 @@ def tile_equilibrium_mass_balance_s3_kernel(
 
         g_q, g_s, f_p, f_sp, g_i = {}, {}, {}, {}, {}
 
-        def g_lay(u, first, last, eng, tiles=4):
+        def g_lay(u, first, last, eng):
             if u not in g_i:
                 g_i[u] = lay("g", u)
             ms = slice(8 * first, 8 * last)
             copy = nc.scalar.copy if eng == "s" else nc.vector.tensor_copy
             copy(
-                g_i[u][:].rearrange("p (t a b) j -> p a j b t", t=4, b=2)[:, ms, :, :, :tiles],
-                g_sb[u][:].rearrange("p j (a b t) -> p a j b t", t=4, b=2)[:, ms, :, :, :tiles],
+                g_i[u][:].rearrange("p (t a b) j -> p a j b t", t=4, b=2)[:, ms],
+                g_sb[u][:].rearrange("p j (a b t) -> p a j b t", t=4, b=2)[:, ms],
             )
 
-        def g_lay_t(u, i, eng):
+        def g_lay_pool(u, first, last):
             if u not in g_i:
                 g_i[u] = lay("g", u)
-            ts = slice(i[0], i[-1] + 1)
-            dst = g_i[u][:].rearrange("p (t m) j -> p t m j", t=4)[:, ts]
-            src = g_sb[u][:].rearrange("p j (m t) -> p t m j", t=4)[:, ts]
-            if eng == "g":
-                nc.gpsimd.tensor_scalar(out=dst, in0=src, scalar1=1.0, scalar2=0.0, op0=ALU.mult, op1=ALU.add)
-            else:
-                nc.scalar.copy(dst, src)
+            ms = slice(16 * first, 16 * last)
+            nc.gpsimd.tensor_scalar(
+                out=g_i[u][:].rearrange("p (t m) j -> p t m j", t=4)[:, :, ms],
+                in0=g_sb[u][:].rearrange("p j (m t) -> p t m j", t=4)[:, :, ms],
+                scalar1=1.0, scalar2=0.0, op0=ALU.mult, op1=ALU.add,
+            )
 
         def g_quant(u):
             g_q[u], g_s[u] = quantise("g%d" % u, g_i[u])
@@ -387,11 +386,10 @@ def tile_equilibrium_mass_balance_s3_kernel(
         phi_turn(0, 1, 5)
         lam_quant(0, 0)
         phi_copy(0, 0)
-        g_lay(0, 0, 4, "s", 3)
+        g_lay(0, 0, 3, "s")
         phi_copy(0, 1)
-        g_lay(0, 4, 8, "s", 3)
-        g_lay_t(0, (3,), "g")
-        f_scale(0, (1,), "g")
+        g_lay(0, 3, 7, "s")
+        g_lay_pool(0, 7, 8)
         lam_mult(0, 1, 0)
         lam_mult(0, 1, 1)
         z_lams(0, 0, 0)
@@ -399,6 +397,7 @@ def tile_equilibrium_mass_balance_s3_kernel(
         phi_turn(1, 0, 5)
         phi_turn(1, 1, 4)
         f_move(1, 0)
+        f_scale(0, (1,))
         lam_quant(0, 1)
         phi_quant(0)
         g_quant(0)

@@ -1,3 +1,4 @@
+import math
 from contextlib import ExitStack
 
 import concourse.mybir as mybir
@@ -25,11 +26,12 @@ UNITS = S // 512
 LG = E // 512
 FIRST = 2
 NB = 3
+ADD_ORDER = ((2, 0, 3, 1), (0, 1, 2, 3))
 SLOT = {("lam", 0, 0): 0, ("g", 0): 0, ("lam", 1, 0): 0, ("lam", 0, 1): 1, ("g", 1): 5, ("lam", 1, 1): 1,
         ("phi", 0): 2, ("g", 2): 2, ("phi", 1): 3, ("g", 3): 4}
 X, Y = (6, 7, 0, 1), (3, 2, 5, 4)
 ZB = {(0, 0): X, (0, 1): Y, (0, 2): X[2:] + Y[:2], (0, 3): Y[2:] + X[:2], (1, 0): Y, (1, 1): X, (1, 2): Y, (1, 3): X}
-OB = Y + X
+OB = (Y[0], Y[2], Y[1], Y[3], X[0], X[2], X[1], X[3])
 
 
 def tile_equilibrium_mass_balance_s3_kernel(
@@ -212,7 +214,7 @@ def tile_equilibrium_mass_balance_s3_kernel(
                 in_=f_raw[u // 2][:, ks[0] : ks[-1] + 1, 512 * (u % 2) : 512 * (u % 2 + 1)].rearrange("p k (m t) -> p k t m", t=4),
             )
 
-        e_sb, flat, nb, n_q, n_s, z_ps = {}, {}, {}, {}, {}, {}
+        e_sb, flat, nb, n_q, n_s, z_ps, pairs = {}, {}, {}, {}, {}, {}, {}
 
         def z_lam(h, u, t, k, phi_first=False):
             if k == 0 and not phi_first:
@@ -237,25 +239,55 @@ def tile_equilibrium_mass_balance_s3_kernel(
 
         def exp(h, u, t):
             if t == 0:
-                e_sb[h, u] = work.tile([P, 4, HALF], F32, name="e_sb", tag="e_sb", bufs=6)
+                e_sb[h, u] = work.tile([P, 4, HALF], F32, name="e_sb", tag="e_sb", bufs=4)
             nc.scalar.activation(e_sb[h, u][:, t, :], z_ps[h, u, t][:], ACT.Exp)
 
-        def n_scale(h, u, t):
+        def exp_pair(h, u, t):
+            if t == 0:
+                pairs[h, u] = work.tile([P, 2, HALF, 2], BF16, name="pairs", tag="pairs", bufs=4)
+            nc.scalar.activation(
+                pairs[h, u][:, t // 2, :, t % 2], z_ps[h, u, t][:], ACT.Exp, bias=log_m[:, 4 * u + t : 4 * u + t + 1]
+            )
+
+        def n_sign(h, u):
+            nb[h, u] = work.tile([P, HALF, 4], BF16, name="nb", tag="nb", bufs=NB, align_bytes=64)
+            nc.vector.tensor_tensor(
+                out=nb[h, u][:].rearrange("p r (v e) -> p r v e", e=2),
+                in0=pairs[h, u][:].rearrange("p v r e -> p r v e"),
+                in1=sign_m[:, 4 * u : 4 * u + 4].rearrange("p (v e) -> p v e", e=2).unsqueeze(1).to_broadcast([P, HALF, 2, 2]),
+                op=ALU.mult,
+            )
+
+        def small(name, dtype=F32):
+            return keep.tile([P, UNITS * 4], dtype, name=name)
+
+        def small_stt(name, a, number, op0, b, op1):
+            dst = small(name)
+            nc.vector.scalar_tensor_tensor(out=dst[:], in0=a[:], scalar=number, in1=b[:], op0=op0, op1=op1)
+            return dst
+
+        def small_act(name, src, func, dtype=F32, **kw):
+            dst = small(name, dtype)
+            nc.scalar.activation(dst[:], src, func, **kw)
+            return dst
+
+        def n_scale(h, u, t, cells=HALF):
             if t == 0:
                 flat[h, u] = work.tile([P, 4, HALF], BF16, name="flat", tag="wide", bufs=2)
             nc.scalar.activation(
-                flat[h, u][:, t, :], e_sb[h, u][:, t, :], ACT.Copy, scale=m_f[:, 4 * u + t : 4 * u + t + 1]
+                flat[h, u][:, t, :cells], e_sb[h, u][:, t, :cells], ACT.Copy, scale=m_f[:, 4 * u + t : 4 * u + t + 1]
             )
 
-        def n_lay(h, u, eng="v"):
-            nb[h, u] = work.tile([P, HALF, 4], BF16, name="nb", tag="nb", bufs=NB, align_bytes=64)
-            (nc.scalar.copy if eng == "s" else nc.vector.tensor_copy)(
-                nb[h, u][:].rearrange("p (r i) t -> p r t i", i=4),
-                flat[h, u][:].rearrange("p t (r i) -> p r t i", i=4),
+        def n_lay(h, u, cells=HALF):
+            if (h, u) not in nb:
+                nb[h, u] = work.tile([P, HALF, 4], BF16, name="nb", tag="nb", bufs=NB, align_bytes=64)
+            nc.vector.tensor_copy(
+                nb[h, u][:].rearrange("p (r i) t -> p r t i", i=4)[:, : cells // 4],
+                flat[h, u][:].rearrange("p t (r i) -> p r t i", i=4)[:, : cells // 4],
             )
 
         def n_mult(h, u, first=0, last=HALF // 4):
-            if first == 0:
+            if (h, u) not in nb:
                 nb[h, u] = work.tile([P, HALF, 4], BF16, name="nb", tag="nb", bufs=NB, align_bytes=64)
             nc.vector.tensor_tensor(
                 out=nb[h, u][:].rearrange("p (r i) t -> p r t i", i=4)[:, first:last],
@@ -272,13 +304,13 @@ def tile_equilibrium_mass_balance_s3_kernel(
         def balance(h, c, e):
             acc[h, c, e] = bank(OB[2 * c + e])
             cols = slice(128 * c, 128 * (c + 1))
-            for u in (0, 1, 3, 2):
+            for u in ADD_ORDER[h]:
                 nc.tensor.matmul_mx(
                     out=acc[h, c, e][:],
                     lhsT=n_q[h, u][:, cols].bitcast(FP8X4), lhsT_scale=n_s[h, u][:, cols],
                     rhs=a_sb[:, u, 1024 * e : 1024 * (e + 1)].bitcast(FP4X4),
                     rhs_scale=a_sc[:, u, 512 * e : 512 * (e + 1)],
-                    start=(u == 0), stop=(u == 2),
+                    start=(u == ADD_ORDER[h][0]), stop=(u == ADD_ORDER[h][-1]),
                 )
 
         def last_columns(h, c, e, banks):
@@ -308,6 +340,7 @@ def tile_equilibrium_mass_balance_s3_kernel(
                 nc.sync.dma_start(out=out_v[h][:, c, cols], in_=o[:])
 
         FOUR = range(4)
+        APART = (0, 2, 1, 3)
 
         def z_lams(h, u, k, tiles=FOUR):
             for t in tiles:
@@ -317,15 +350,15 @@ def tile_equilibrium_mass_balance_s3_kernel(
             for k in range(LG):
                 z_lam(h, u, t, k)
             z_phi(h, u, t)
-            exp(h, u, t)
+            exp_pair(h, u, t)
 
         def z_unit(h, u):
-            for t in FOUR:
+            for t in APART:
                 z_tile(h, u, t)
 
-        def scale_unit(h, u):
+        def scale_unit(h, u, cells=HALF):
             for t in FOUR:
-                n_scale(h, u, t)
+                n_scale(h, u, t, cells)
 
 
         f_first = scale_tile("f_first", LG, 512 * FIRST)
@@ -356,11 +389,11 @@ def tile_equilibrium_mass_balance_s3_kernel(
         load_lam(1, 0)
         load_scales(f_rest, f_scales[:, :, 512 * FIRST :])
         load_f(0, 1)
+        nc.sync.dma_start(out=m_sb[:], in_=m.rearrange("(u p t) -> p u t", p=P, t=4))
         load_g(2)
         load_f(1, 1)
         load_g(3)
         load_lam(1, 1)
-        nc.sync.dma_start(out=m_sb[:], in_=m.rearrange("(u p t) -> p u t", p=P, t=4))
         load_scales(a_sc, a_scales)
         nc.sync.dma_start(out=a_sb[:], in_=a_v)
 
@@ -423,88 +456,106 @@ def tile_equilibrium_mass_balance_s3_kernel(
             z_phi(0, 1, t)
         lam_turn_whole(1, 0, 0, X[0])
         lam_turn_whole(1, 0, 1, X[1])
+        m_all = m_sb[:].rearrange("p u t -> p (u t)")
+        m_abs = small_act("m_abs", m_all, ACT.Abs)
+        sign_m = small_act("sign_m", m_all, ACT.Sign, BF16)
+        size = small("size")
         g_lay(2, 0, 4, "s")
         f_scale(2, (0, 1))
         f_move(1, 2, 2)
         g_lay(2, 4, 8, "v")
-        for t in FOUR:
-            exp(0, 1, t)
         f_scale(3, (1,))
+        nc.vector.tensor_scalar(out=size[:], in0=m_abs[:], scalar1=2.0**-126, scalar2=None, op0=ALU.max)
+        for t in (0, 1, 2):
+            exp(0, 1, t)
+        guess = small_act(
+            "guess", size[:].bitcast(U32), ACT.Copy, scale=-math.log(2.0) / 2**23, bias=math.log(2.0) * (127 - 0.043) + 1.5
+        )
+        exp(0, 1, 3)
+        back = small_act("back", guess[:], ACT.Exp, bias=-1.5)
         g_quant(2)
         f_scale(3, (0,), "g", ("g", 2))
         lam_mult(1, 0, 0)
         lam_mult(1, 0, 1)
+        ratio = small("ratio")
+        nc.vector.tensor_tensor(out=ratio[:], in0=back[:], in1=size[:], op=ALU.mult)
         for t in FOUR:
             for k in range(LG):
                 z_lam(0, 2, t, k)
         g_lay(3, 0, 5, "s")
-        for t in FOUR:
+        g_lay(3, 5, 8, "v")
+        bend = small_stt("bend", ratio, 4.0, ALU.subtract, ratio, ALU.mult)
+        nc.vector.tensor_copy(out=m_f[:], in_=m_sb[:].rearrange("p u t -> p (u t)"))
+        closer = small_stt("closer", bend, 0.5, ALU.mult, guess, ALU.add)
+        z_phi(0, 2, 0)
+        exp(0, 2, 0)
+        back2 = small_act("back2", closer[:], ACT.Exp)
+        for t in (1, 2, 3):
             z_phi(0, 2, t)
             exp(0, 2, t)
-        g_lay(3, 5, 8, "v")
         for i in FOUR:
             load_feed(i // 2, i % 2)
-        nc.vector.tensor_copy(out=m_f[:], in_=m_sb[:].rearrange("p u t -> p (u t)"))
         g_quant(3)
         lam_spread(1, 1)
+        ratio2 = small("ratio2")
+        nc.vector.tensor_tensor(out=ratio2[:], in0=back2[:], in1=size[:], op=ALU.mult)
         phi_quant(1)
+        log_m = small_stt("log_m", ratio2, 1.0, ALU.subtract, closer, ALU.subtract)
         lam_quant(1, 0)
         for t in FOUR:
             for k in range(LG):
                 z_lam(0, 3, t, k)
         for t in FOUR:
             z_phi(0, 3, t)
-        exp(0, 3, 0)
         for t in FOUR:
-            if t < 3:
-                exp(0, 3, t + 1)
-            n_scale(0, 0, t)
+            exp(0, 3, t)
+        scale_unit(0, 0)
         lam_turn_whole(1, 1, 0, X[2])
         lam_turn_whole(1, 1, 1, X[3])
         lam_mult(1, 1, 0)
         lam_mult(1, 1, 1)
-        for h, u, t in ((1, 0, 0), (1, 0, 1), (1, 0, 2), (1, 0, 3), (1, 1, 0), (1, 1, 1)):
+        for h, u, t in ((1, 0, 0), (1, 0, 2), (1, 0, 1), (1, 0, 3), (1, 1, 0), (1, 1, 2)):
             z_phi(h, u, t, True)
             z_lam(h, u, t, 0, True)
-        scale_unit(0, 1)
         lam_quant(1, 1)
         n_mult(0, 2)
+        scale_unit(0, 1)
         n_lay(0, 0)
-        for t in FOUR:
-            z_lam(1, 0, t, 1, True)
-            exp(1, 0, t)
-        for t in (0, 1):
-            z_lam(1, 1, t, 1, True)
-            exp(1, 1, t)
         n_quant(0, 2)
+        for t in APART:
+            z_lam(1, 0, t, 1, True)
+            exp_pair(1, 0, t)
+        for t in (0, 2):
+            z_lam(1, 1, t, 1, True)
+            exp_pair(1, 1, t)
         n_mult(0, 3)
         n_quant(0, 0)
-        z_tile(1, 1, 2)
-        z_tile(1, 1, 3)
         n_lay(0, 1)
         n_quant(0, 3)
         n_quant(0, 1)
-        n_mult(1, 0)
-        for t in FOUR:
-            z_tile(1, 2, t)
-            n_scale(1, 1, t)
+        n_sign(1, 0)
+        z_tile(1, 1, 1)
+        z_tile(1, 1, 3)
+        z_unit(1, 2)
         z_unit(1, 3)
-        scale_unit(1, 2)
-        n_lay(1, 1)
+        n_sign(1, 1)
         n_quant(1, 0)
         for c in FOUR:
             for e in range(2):
                 balance(0, c, e)
         n_quant(1, 1)
-        n_mult(1, 3)
-        n_lay(1, 2)
-        n_quant(1, 3)
         finish(0, 0, 0)
+        n_sign(1, 2)
+        finish(0, 0, 1)
         n_quant(1, 2)
-        for c in FOUR:
-            for e in range(2):
-                if (c, e) != (0, 0):
-                    finish(0, c, e)
+        finish(0, 1, 0)
+        finish(0, 1, 1)
+        n_sign(1, 3)
+        finish(0, 2, 0)
+        n_quant(1, 3)
+        finish(0, 2, 1)
+        finish(0, 3, 0)
+        finish(0, 3, 1)
         for c in FOUR:
             for e in range(2):
                 balance(1, c, e)

@@ -27,11 +27,12 @@ LG = E // 512
 FIRST = 2
 NB = 3
 ADD_ORDER = ((2, 0, 3, 1), (0, 1, 2, 3))
-SLOT = {("lam", 0, 0): 0, ("g", 0): 0, ("lam", 1, 0): 0, ("lam", 0, 1): 1, ("g", 1): 5, ("lam", 1, 1): 1,
-        ("phi", 0): 2, ("g", 2): 2, ("phi", 1): 3, ("g", 3): 4}
+SLOT = {("lam", 0, 0): 0, ("g", 0): 4, ("lam", 1, 0): 0, ("lam", 0, 1): 1, ("g", 1): 5, ("lam", 1, 1): 1,
+        ("phi", 0): 2, ("g", 2): 2, ("phi", 1): 3, ("g", 3): 2}
 X, Y = (6, 7, 0, 1), (3, 2, 5, 4)
-ZB = {(0, 0): X, (0, 1): Y, (0, 2): X[2:] + Y[:2], (0, 3): Y[2:] + X[:2], (1, 0): Y, (1, 1): X, (1, 2): Y, (1, 3): X}
-OB = (Y[0], Y[2], Y[1], Y[3], X[0], X[2], X[1], X[3])
+YA, XA = (Y[0], Y[2], Y[1], Y[3]), (X[0], X[2], X[1], X[3])
+ZB = {(0, 0): X, (0, 1): Y, (0, 2): X[2:] + Y[:2], (0, 3): Y[2:] + X[:2], (1, 0): YA, (1, 1): XA, (1, 2): YA, (1, 3): XA}
+OB = Y + X
 
 
 def tile_equilibrium_mass_balance_s3_kernel(
@@ -62,6 +63,12 @@ def tile_equilibrium_mass_balance_s3_kernel(
         def load_lam(h, k):
             lam_sb[h, k] = keep.tile([P, ROWS, 512], U8, name="lam_sb%d%d" % (h, k))
             nc.sync.dma_start(out=lam_sb[h, k][:], in_=lam_v[h][:, :, 512 * k : 512 * (k + 1)])
+
+        def load_lam_rows(pair):
+            lam_sb[0, "rows", pair] = keep.tile([P, 2 * E], U8, name="lam_rows%d" % pair)
+            nc.sync.dma_start(
+                out=lam_sb[0, "rows", pair][:], in_=lam_v[0][:, 2 * pair : 2 * pair + 2].rearrange("p c k -> p (c k)")
+            )
 
         def load_phi(h, pair):
             phi_sb[h, pair] = keep.tile([P, 2 * D], BF16, name="phi_sb%d%d" % (h, pair))
@@ -96,7 +103,7 @@ def tile_equilibrium_mass_balance_s3_kernel(
             if (h, k) not in wide:
                 wide[h, k] = work.tile([P, ROWS * 512], BF16, name="wide", tag="wide", bufs=2)
             copy = nc.scalar.copy if eng == "s" else nc.vector.tensor_copy
-            copy(wide[h, k][:, 512 * c : 512 * (c + 1)], lam_sb[h, k][:, c, :].bitcast(FP8))
+            copy(wide[h, k][:, 512 * c : 512 * (c + 1)], lam_sb[h, "rows", c // 2][:, E * (c % 2) + 512 * k : E * (c % 2) + 512 * (k + 1)].bitcast(FP8))
 
         def turn(key, rows, pair, b):
             turned[key] = bank(b)
@@ -109,11 +116,13 @@ def tile_equilibrium_mass_balance_s3_kernel(
                         turned[key][:, at : at + 128], words[:, 256 * c + u : 256 * (c + 1) : 2], ident[:]
                     )
 
-        def lam_spread(h, k):
-            wide[h, k] = work.tile([P, ROWS * 512], BF16, name="wide", tag="wide", bufs=2)
+        def lam_spread(h, k, first=0, last=2):
+            if first == 0:
+                wide[h, k] = work.tile([P, ROWS * 512], BF16, name="wide", tag="wide", bufs=2)
+            ws = slice(256 * first, 256 * last)
             nc.vector.tensor_scalar(
-                out=wide[h, k][:].rearrange("p (u w e) -> p w u e", u=2, e=2),
-                in0=lam_sb[h, k][:].rearrange("p c k -> p (c k)").bitcast(FP8).rearrange("p (w u e) -> p w u e", u=2, e=2),
+                out=wide[h, k][:].rearrange("p (u w e) -> p w u e", u=2, e=2)[:, ws],
+                in0=lam_sb[h, k][:].rearrange("p c k -> p (c k)").bitcast(FP8).rearrange("p (w u e) -> p w u e", u=2, e=2)[:, ws],
                 scalar1=one[:], scalar2=None, op0=ALU.mult,
             )
 
@@ -301,10 +310,11 @@ def tile_equilibrium_mass_balance_s3_kernel(
 
         acc = {}
 
-        def balance(h, c, e):
-            acc[h, c, e] = bank(OB[2 * c + e])
+        def balance(h, c, e, first=0, last=UNITS):
+            if first == 0:
+                acc[h, c, e] = bank(OB[2 * c + e])
             cols = slice(128 * c, 128 * (c + 1))
-            for u in ADD_ORDER[h]:
+            for u in ADD_ORDER[h][first:last]:
                 nc.tensor.matmul_mx(
                     out=acc[h, c, e][:],
                     lhsT=n_q[h, u][:, cols].bitcast(FP8X4), lhsT_scale=n_s[h, u][:, cols],
@@ -374,17 +384,17 @@ def tile_equilibrium_mass_balance_s3_kernel(
         one = keep.tile([P, 1], F32, name="one")
         nc.vector.memset(one[:], 1.0)
 
-        load_lam(0, 0)
+        load_lam_rows(0)
         load_f(0, 0)
+        load_lam_rows(1)
         nc.sync.dma_start(out=l_sc[:], in_=lam_scale.rearrange("o (k p t) -> p (o k) t", p=P, t=4))
-        load_lam(0, 1)
         load_scales(f_first, f_scales[:, :, : 512 * FIRST])
         load_phi(0, 0)
         load_phi(0, 1)
         load_g(0)
-        load_f(1, 0)
         load_phi(1, 0)
         load_phi(1, 1)
+        load_f(1, 0)
         load_g(1)
         load_lam(1, 0)
         load_scales(f_rest, f_scales[:, :, 512 * FIRST :])
@@ -397,58 +407,55 @@ def tile_equilibrium_mass_balance_s3_kernel(
         load_scales(a_sc, a_scales)
         nc.sync.dma_start(out=a_sb[:], in_=a_v)
 
-        warm_up(3, 6)
+        warm_up(2, 4)
         lam_cast(0, 0, 0, "v")
         lam_cast(0, 0, 1, "v")
+        lam_cast(0, 1, 0, "s")
+        lam_cast(0, 1, 1, "s")
         lam_cast(0, 0, 2, "s")
         lam_cast(0, 0, 3, "s")
-        lam_turn(0, 0, 0, 0)
-        lam_turn(0, 0, 1, 1)
-        warm_up(2, 6)
+        lam_turn(0, 0, 0, 6)
+        lam_turn(0, 1, 0, 7)
+        warm_up(2, 4)
+        lam_turn(0, 0, 1, 3)
         f_move(0, 0, 2)
         f_scale(0, (0,), "g")
-        for c in FOUR:
-            lam_cast(0, 1, c, "s")
+        lam_cast(0, 1, 2, "s")
+        lam_cast(0, 1, 3, "s")
         lam_mult(0, 0, 0)
+        lam_mult(0, 1, 0)
         lam_mult(0, 0, 1)
         f_scale(1, (0,))
-        lam_turn(0, 1, 0, 2)
-        warm_up(1, 6)
-        phi_turn(0, 0, 3)
-        lam_turn(0, 1, 1, 4)
-        phi_turn(0, 1, 5)
-        lam_quant(0, 0)
-        phi_copy(0, 0)
-        g_lay(0, 0, 3, "s")
-        phi_copy(0, 1)
-        g_lay(0, 3, 7, "s")
-        g_lay_pool(0, 7, 8)
-        lam_mult(0, 1, 0)
-        lam_mult(0, 1, 1)
-        z_lams(0, 0, 0)
-        z_lams(0, 1, 0, (0, 1))
+        phi_turn(0, 0, 0)
+        phi_turn(0, 1, 1)
+        lam_turn(0, 1, 1, 2)
+        warm_up(2, 6)
         phi_turn(1, 0, 5)
         phi_turn(1, 1, 4)
+        lam_quant(0, 0)
+        phi_copy(0, 0)
+        phi_copy(0, 1)
+        g_lay(0, 0, 4, "s")
+        phi_copy(1, 0)
+        phi_copy(1, 1)
+        g_lay(0, 4, 8, "s")
+        lam_mult(0, 1, 1)
+        z_lams(0, 0, 0)
+        z_lams(0, 1, 0)
         f_move(1, 0)
         f_scale(0, (1,))
         lam_quant(0, 1)
         phi_quant(0)
         g_quant(0)
         z_lams(0, 0, 1)
-        g_lay(1, 0, 4, "s")
-        phi_copy(1, 0)
-        phi_copy(1, 1)
-        g_lay(1, 4, 6, "s")
+        g_lay(1, 0, 7, "s")
         f_move(1, 1)
         f_scale(1, (1,))
         for t in FOUR:
             z_phi(0, 0, t)
             exp(0, 0, t)
-        z_lams(0, 1, 1, (0, 1))
-        for t in (2, 3):
-            for k in range(LG):
-                z_lam(0, 1, t, k)
-        g_lay(1, 6, 8, "v")
+        z_lams(0, 1, 1)
+        g_lay(1, 7, 8, "v")
         lam_spread(1, 0)
         g_quant(1)
         f_move(0, 2, 2)
@@ -464,7 +471,7 @@ def tile_equilibrium_mass_balance_s3_kernel(
         f_scale(2, (0, 1))
         f_move(1, 2, 2)
         g_lay(2, 4, 8, "v")
-        f_scale(3, (1,))
+        f_scale(3, (0, 1))
         nc.vector.tensor_scalar(out=size[:], in0=m_abs[:], scalar1=2.0**-126, scalar2=None, op0=ALU.max)
         for t in (0, 1, 2):
             exp(0, 1, t)
@@ -474,7 +481,7 @@ def tile_equilibrium_mass_balance_s3_kernel(
         exp(0, 1, 3)
         back = small_act("back", guess[:], ACT.Exp, bias=-1.5)
         g_quant(2)
-        f_scale(3, (0,), "g", ("g", 2))
+        g_lay_pool(3, 5, 8)
         lam_mult(1, 0, 0)
         lam_mult(1, 0, 1)
         ratio = small("ratio")
@@ -482,14 +489,13 @@ def tile_equilibrium_mass_balance_s3_kernel(
         for t in FOUR:
             for k in range(LG):
                 z_lam(0, 2, t, k)
-        g_lay(3, 0, 5, "s")
-        g_lay(3, 5, 8, "v")
+        g_lay(3, 0, 4, "s")
+        g_lay(3, 4, 5, "v")
         bend = small_stt("bend", ratio, 4.0, ALU.subtract, ratio, ALU.mult)
         nc.vector.tensor_copy(out=m_f[:], in_=m_sb[:].rearrange("p u t -> p (u t)"))
         closer = small_stt("closer", bend, 0.5, ALU.mult, guess, ALU.add)
         z_phi(0, 2, 0)
         exp(0, 2, 0)
-        back2 = small_act("back2", closer[:], ACT.Exp)
         for t in (1, 2, 3):
             z_phi(0, 2, t)
             exp(0, 2, t)
@@ -497,10 +503,7 @@ def tile_equilibrium_mass_balance_s3_kernel(
             load_feed(i // 2, i % 2)
         g_quant(3)
         lam_spread(1, 1)
-        ratio2 = small("ratio2")
-        nc.vector.tensor_tensor(out=ratio2[:], in0=back2[:], in1=size[:], op=ALU.mult)
         phi_quant(1)
-        log_m = small_stt("log_m", ratio2, 1.0, ALU.subtract, closer, ALU.subtract)
         lam_quant(1, 0)
         for t in FOUR:
             for k in range(LG):
@@ -509,15 +512,19 @@ def tile_equilibrium_mass_balance_s3_kernel(
             z_phi(0, 3, t)
         for t in FOUR:
             exp(0, 3, t)
+        back2 = small_act("back2", closer[:], ACT.Exp)
         scale_unit(0, 0)
         lam_turn_whole(1, 1, 0, X[2])
         lam_turn_whole(1, 1, 1, X[3])
         lam_mult(1, 1, 0)
         lam_mult(1, 1, 1)
-        for h, u, t in ((1, 0, 0), (1, 0, 2), (1, 0, 1), (1, 0, 3), (1, 1, 0), (1, 1, 2)):
+        ratio2 = small("ratio2")
+        nc.vector.tensor_tensor(out=ratio2[:], in0=back2[:], in1=size[:], op=ALU.mult)
+        for h, u, t in [(1, u, t) for u in range(2) for t in APART]:
             z_phi(h, u, t, True)
             z_lam(h, u, t, 0, True)
         lam_quant(1, 1)
+        log_m = small_stt("log_m", ratio2, 1.0, ALU.subtract, closer, ALU.subtract)
         n_mult(0, 2)
         scale_unit(0, 1)
         n_lay(0, 0)
@@ -525,7 +532,7 @@ def tile_equilibrium_mass_balance_s3_kernel(
         for t in APART:
             z_lam(1, 0, t, 1, True)
             exp_pair(1, 0, t)
-        for t in (0, 2):
+        for t in APART:
             z_lam(1, 1, t, 1, True)
             exp_pair(1, 1, t)
         n_mult(0, 3)
@@ -534,8 +541,6 @@ def tile_equilibrium_mass_balance_s3_kernel(
         n_quant(0, 3)
         n_quant(0, 1)
         n_sign(1, 0)
-        z_tile(1, 1, 1)
-        z_tile(1, 1, 3)
         z_unit(1, 2)
         z_unit(1, 3)
         n_sign(1, 1)
@@ -549,14 +554,18 @@ def tile_equilibrium_mass_balance_s3_kernel(
         finish(0, 0, 1)
         n_quant(1, 2)
         finish(0, 1, 0)
-        finish(0, 1, 1)
         n_sign(1, 3)
-        finish(0, 2, 0)
+        finish(0, 1, 1)
         n_quant(1, 3)
-        finish(0, 2, 1)
-        finish(0, 3, 0)
-        finish(0, 3, 1)
-        for c in FOUR:
+        for c in (2, 3):
+            for e in range(2):
+                finish(0, c, e)
+        for e in range(2):
+            balance(1, 0, e, 0, UNITS - 1)
+        for e in range(2):
+            balance(1, 0, e, UNITS - 1)
+            finish(1, 0, e)
+        for c in (1, 2, 3):
             for e in range(2):
                 balance(1, c, e)
                 finish(1, c, e, 2 if (c, e) == (3, 1) else 1)

@@ -531,7 +531,7 @@ def tile_equilibrium_mass_balance_s3_kernel(
         n_quant(0, 2)
         for t in APART:
             z_lam(1, 0, t, 1, True)
-            exp_pair(1, 0, t)
+            exp(1, 0, t)
         for t in APART:
             z_lam(1, 1, t, 1, True)
             exp_pair(1, 1, t)
@@ -540,7 +540,7 @@ def tile_equilibrium_mass_balance_s3_kernel(
         n_lay(0, 1)
         n_quant(0, 3)
         n_quant(0, 1)
-        n_sign(1, 0)
+        n_mult(1, 0)
         z_unit(1, 2)
         z_unit(1, 3)
         n_sign(1, 1)

@@ -26,13 +26,15 @@ UNITS = S // 512
 LG = E // 512
 FIRST = 2
 NB = 3
+REGION = {"moving scales": 0, "moving codes": 7168 + 128, "stationary": 7168 + 128 + 20480 + 64}
 ADD_ORDER = ((2, 0, 3, 1), (0, 1, 2, 3))
 SLOT = {("lam", 0, 0): 0, ("g", 0): 4, ("lam", 1, 0): 0, ("lam", 0, 1): 1, ("g", 1): 5, ("lam", 1, 1): 1,
         ("phi", 0): 2, ("g", 2): 2, ("phi", 1): 3, ("g", 3): 2}
 X, Y = (6, 7, 0, 1), (3, 2, 5, 4)
-YA, XA = (Y[0], Y[2], Y[1], Y[3]), (X[0], X[2], X[1], X[3])
-ZB = {(0, 0): X, (0, 1): Y, (0, 2): X[2:] + Y[:2], (0, 3): Y[2:] + X[:2], (1, 0): YA, (1, 1): XA, (1, 2): YA, (1, 3): XA}
-OB = Y + X
+XR = X[2:] + X[:2]
+YA, XA = (Y[0], Y[2], Y[1], Y[3]), (XR[0], XR[2], XR[1], XR[3])
+ZB = {(0, 0): X, (0, 1): Y, (0, 2): X[:2] + Y[:2], (0, 3): Y[2:] + X[2:], (1, 0): YA, (1, 1): XA, (1, 2): YA, (1, 3): XA}
+OB = Y + XR
 
 
 def tile_equilibrium_mass_balance_s3_kernel(
@@ -42,6 +44,7 @@ def tile_equilibrium_mass_balance_s3_kernel(
     with ExitStack() as ctx:
         keep = ctx.enter_context(tc.tile_pool(name="keep", bufs=1))
         work = ctx.enter_context(tc.tile_pool(name="work", bufs=2))
+        mx = ctx.enter_context(tc.tile_pool(name="mx", bufs=1))
         psum = ctx.enter_context(tc.psum_pool(name="psum", bufs=1))
         ctx.enter_context(tc.manual_schedule())
 
@@ -51,6 +54,13 @@ def tile_equilibrium_mass_balance_s3_kernel(
         out_v = out.rearrange("(h p c) e -> h p c e", h=2, c=ROWS)
         g_v = g.rearrange("(p j) s -> p j s", j=4)
         a_v = a_words.rearrange("k p b -> p k b")
+
+        cursor = dict(REGION)
+
+        def operand(region, shape, dtype, size, name):
+            at = cursor[region]
+            cursor[region] = at + size
+            return mx.tile(shape, dtype, name=name, offset=at, align_bytes=256 if at == 0 else 64)
 
         def bank(i):
             return psum.tile([P, 512], F32, name="bank%d" % i)
@@ -134,11 +144,12 @@ def tile_equilibrium_mass_balance_s3_kernel(
                     at, src = 256 * u + 128 * i, 512 * u + 128 * (2 * pair + i)
                     nc.tensor.transpose(turned[h, k, pair][:, at : at + 128], words[:, src : src + 128], ident[:])
 
-        def warm_up(blocks, b):
+        def warm_up(cols, b):
             idle = bank(b)
+            width = min(cols, P)
             nc.tensor.matmul(
-                idle[:, : P * blocks].rearrange("p (b n) -> p b n", n=P), lhsT=ident[:],
-                rhs=ident[:].unsqueeze(1).to_broadcast([P, blocks, P]), start=True, stop=True,
+                idle[:, :cols].rearrange("p (b n) -> p b n", n=width), lhsT=ident[:],
+                rhs=ident[:, :width].unsqueeze(1).to_broadcast([P, cols // width, width]), start=True, stop=True,
             )
 
         def lam_turn(h, k, pair, b):
@@ -165,17 +176,17 @@ def tile_equilibrium_mass_balance_s3_kernel(
                 dst[:, 256 * pair : 256 * (pair + 1)], turned[h, "phi", pair][:].rearrange("p (u r) -> p r u", u=2)
             )
 
-        def quantise(name, src):
-            codes = keep.tile([P, 512], U32, name=name + "_q", align_bytes=64)
-            scales = keep.tile([P, 512], U8, name=name + "_s", align_bytes=64)
+        def quantise(name, src, moving=False):
+            codes = operand("moving codes" if moving else "stationary", [P, 512], U32, 2048, name + "_q")
+            scales = operand("moving scales" if moving else "stationary", [P, 512], U8, 512, name + "_s")
             nc.vector.quantize_mx(out=codes[:].bitcast(FP8X4), scales=scales[:], in_=src[:].rearrange("p r t -> p (r t)"))
             return codes, scales
 
         def phi_quant(h):
-            phi_q[h], phi_s[h] = quantise("phi%d" % h, phi_t[h])
+            phi_q[h], phi_s[h] = quantise("phi%d" % h, phi_t[h], True)
 
         def lam_quant(h, k):
-            lam_q[h, k], lam_s[h, k] = quantise("lam%d%d" % (h, k), lam_t[h, k])
+            lam_q[h, k], lam_s[h, k] = quantise("lam%d%d" % (h, k), lam_t[h, k], True)
 
         g_q, g_s, f_p, f_sp, g_i = {}, {}, {}, {}, {}
 
@@ -205,7 +216,7 @@ def tile_equilibrium_mass_balance_s3_kernel(
         def f_move(k, first, count=1):
             pair, at = divmod(first, 2)
             if (k, pair) not in f_p:
-                f_p[k, pair] = keep.tile([P, 2, 1024], U8, name="f_p%d%d" % (k, pair), align_bytes=64)
+                f_p[k, pair] = operand("stationary", [P, 2, 1024], U8, 2048, "f_p%d%d" % (k, pair))
             nc.vector.tensor_copy(
                 out=f_p[k, pair][:, at : at + count].bitcast(U16).rearrange("p u (t m) -> p u t m", t=4),
                 in_=f_sb[k, pair][:].bitcast(U16).rearrange("p (u m t) -> p u t m", u=2, t=4)[:, at : at + count],
@@ -213,7 +224,7 @@ def tile_equilibrium_mass_balance_s3_kernel(
 
         def f_scale(u, ks, eng="v", slot=None):
             if slot is None:
-                dst = keep.tile([P, len(ks), 512], U8, name="f_sp%d%d" % (u, ks[0]), align_bytes=64)[:]
+                dst = operand("stationary", [P, len(ks), 512], U8, 512 * len(ks), "f_sp%d%d" % (u, ks[0]))[:]
             else:
                 dst = lay(*slot)[:].rearrange("p r t -> p (r t)")[:, : 256 * len(ks)].bitcast(U8).rearrange("p (k n) -> p k n", n=512)
             for i, k in enumerate(ks):
@@ -337,7 +348,7 @@ def tile_equilibrium_mass_balance_s3_kernel(
                     )
                 o = work.tile([P, P], F32, name="o", tag="o", bufs=10)
                 nc.vector.tensor_tensor(out=o[:], in0=part[:, :P], in1=feed_sb[h, c // 2][:, c % 2, at : at + P], op=ALU.subtract)
-                nc.sync.dma_start(out=out_v[h][:, c, at : at + P], in_=o[:])
+                (nc.scalar if i % 2 == 0 else nc.sync).dma_start(out=out_v[h][:, c, at : at + P], in_=o[:])
 
         def finish(h, c, e, parts=1):
             w = 512 // parts
@@ -376,11 +387,12 @@ def tile_equilibrium_mass_balance_s3_kernel(
         make_identity(nc, ident[:])
         f_rest = scale_tile("f_rest", LG, S - 512 * FIRST)
         f_raw[0], f_raw[1] = f_first, f_rest
-        a_sc = scale_tile("a_sc", UNITS, E)
+        a_sc = operand("moving scales", [P, UNITS, E], U8, UNITS * E, "a_sc")
+        nc.vector.memset(a_sc[:].bitcast(I32), 0)
         l_sc = keep.tile([P, LG, 4], F32, name="l_sc")
         m_sb = keep.tile([P, UNITS, 4], BF16, name="m_sb")
         m_f = keep.tile([P, UNITS * 4], F32, name="m_f")
-        a_sb = keep.tile([P, UNITS, 2 * E], U8, name="a_sb", align_bytes=64)
+        a_sb = operand("moving codes", [P, UNITS, 2 * E], U8, UNITS * 2 * E, "a_sb")
         one = keep.tile([P, 1], F32, name="one")
         nc.vector.memset(one[:], 1.0)
 
@@ -407,7 +419,7 @@ def tile_equilibrium_mass_balance_s3_kernel(
         load_scales(a_sc, a_scales)
         nc.sync.dma_start(out=a_sb[:], in_=a_v)
 
-        warm_up(2, 4)
+        warm_up(384, 4)
         lam_cast(0, 0, 0, "v")
         lam_cast(0, 0, 1, "v")
         lam_cast(0, 1, 0, "s")
@@ -416,20 +428,21 @@ def tile_equilibrium_mass_balance_s3_kernel(
         lam_cast(0, 0, 3, "s")
         lam_turn(0, 0, 0, 6)
         lam_turn(0, 1, 0, 7)
-        warm_up(2, 4)
+        warm_up(256, 4)
         lam_turn(0, 0, 1, 3)
         f_move(0, 0, 2)
         f_scale(0, (0,), "g")
+        f_scale(1, (0,), "g")
         lam_cast(0, 1, 2, "s")
         lam_cast(0, 1, 3, "s")
         lam_mult(0, 0, 0)
         lam_mult(0, 1, 0)
         lam_mult(0, 0, 1)
-        f_scale(1, (0,))
+        f_scale(0, (1,))
         phi_turn(0, 0, 0)
         phi_turn(0, 1, 1)
         lam_turn(0, 1, 1, 2)
-        warm_up(2, 6)
+        warm_up(128, 6)
         phi_turn(1, 0, 5)
         phi_turn(1, 1, 4)
         lam_quant(0, 0)
@@ -443,26 +456,22 @@ def tile_equilibrium_mass_balance_s3_kernel(
         z_lams(0, 0, 0)
         z_lams(0, 1, 0)
         f_move(1, 0)
-        f_scale(0, (1,))
         lam_quant(0, 1)
         phi_quant(0)
         g_quant(0)
         z_lams(0, 0, 1)
-        g_lay(1, 0, 7, "s")
+        g_lay(1, 0, 6, "s")
         f_move(1, 1)
         f_scale(1, (1,))
         for t in FOUR:
             z_phi(0, 0, t)
             exp(0, 0, t)
         z_lams(0, 1, 1)
-        g_lay(1, 7, 8, "v")
-        lam_spread(1, 0)
-        g_quant(1)
+        g_lay(1, 6, 8, "v")
         f_move(0, 2, 2)
+        g_quant(1)
         for t in FOUR:
             z_phi(0, 1, t)
-        lam_turn_whole(1, 0, 0, X[0])
-        lam_turn_whole(1, 0, 1, X[1])
         m_all = m_sb[:].rearrange("p u t -> p (u t)")
         m_abs = small_act("m_abs", m_all, ACT.Abs)
         sign_m = small_act("sign_m", m_all, ACT.Sign, BF16)
@@ -470,6 +479,12 @@ def tile_equilibrium_mass_balance_s3_kernel(
         g_lay(2, 0, 4, "s")
         f_scale(2, (0, 1))
         f_move(1, 2, 2)
+        lam_spread(1, 0)
+        for t in (0, 1):
+            for k in range(LG):
+                z_lam(0, 2, t, k)
+        lam_turn_whole(1, 0, 0, X[2])
+        lam_turn_whole(1, 0, 1, X[3])
         g_lay(2, 4, 8, "v")
         f_scale(3, (0, 1))
         nc.vector.tensor_scalar(out=size[:], in0=m_abs[:], scalar1=2.0**-126, scalar2=None, op0=ALU.max)
@@ -486,14 +501,12 @@ def tile_equilibrium_mass_balance_s3_kernel(
         lam_mult(1, 0, 1)
         ratio = small("ratio")
         nc.vector.tensor_tensor(out=ratio[:], in0=back[:], in1=size[:], op=ALU.mult)
-        for t in FOUR:
+        for t in (2, 3):
             for k in range(LG):
                 z_lam(0, 2, t, k)
         g_lay(3, 0, 4, "s")
         g_lay(3, 4, 5, "v")
-        bend = small_stt("bend", ratio, 4.0, ALU.subtract, ratio, ALU.mult)
         nc.vector.tensor_copy(out=m_f[:], in_=m_sb[:].rearrange("p u t -> p (u t)"))
-        closer = small_stt("closer", bend, 0.5, ALU.mult, guess, ALU.add)
         z_phi(0, 2, 0)
         exp(0, 2, 0)
         for t in (1, 2, 3):
@@ -502,6 +515,7 @@ def tile_equilibrium_mass_balance_s3_kernel(
         for i in FOUR:
             load_feed(i // 2, i % 2)
         g_quant(3)
+        bend = small_stt("bend", ratio, 4.0, ALU.subtract, ratio, ALU.mult)
         lam_spread(1, 1)
         phi_quant(1)
         lam_quant(1, 0)
@@ -512,21 +526,25 @@ def tile_equilibrium_mass_balance_s3_kernel(
             z_phi(0, 3, t)
         for t in FOUR:
             exp(0, 3, t)
-        back2 = small_act("back2", closer[:], ACT.Exp)
         scale_unit(0, 0)
-        lam_turn_whole(1, 1, 0, X[2])
-        lam_turn_whole(1, 1, 1, X[3])
+        lam_turn_whole(1, 1, 0, X[0])
+        lam_turn_whole(1, 1, 1, X[1])
         lam_mult(1, 1, 0)
         lam_mult(1, 1, 1)
-        ratio2 = small("ratio2")
-        nc.vector.tensor_tensor(out=ratio2[:], in0=back2[:], in1=size[:], op=ALU.mult)
+        closer = small_stt("closer", bend, 0.5, ALU.mult, guess, ALU.add)
         for h, u, t in [(1, u, t) for u in range(2) for t in APART]:
             z_phi(h, u, t, True)
             z_lam(h, u, t, 0, True)
         lam_quant(1, 1)
+        n_mult(0, 2, 0, 64)
+        n_scale(0, 1, 0)
+        back2 = small_act("back2", closer[:], ACT.Exp)
+        for t in (1, 2, 3):
+            n_scale(0, 1, t)
+        ratio2 = small("ratio2")
+        nc.vector.tensor_tensor(out=ratio2[:], in0=back2[:], in1=size[:], op=ALU.mult)
+        n_mult(0, 2, 64, 128)
         log_m = small_stt("log_m", ratio2, 1.0, ALU.subtract, closer, ALU.subtract)
-        n_mult(0, 2)
-        scale_unit(0, 1)
         n_lay(0, 0)
         n_quant(0, 2)
         for t in APART:
@@ -567,5 +585,7 @@ def tile_equilibrium_mass_balance_s3_kernel(
             finish(1, 0, e)
         for c in (1, 2, 3):
             for e in range(2):
-                balance(1, c, e)
-                finish(1, c, e, 2 if (c, e) == (3, 1) else 1)
+                if (c, e) != (3, 1):
+                    balance(1, c, e)
+                    finish(1, c, e)
+        last_columns(1, 3, 1, (OB[7], OB[0], OB[1], OB[2]))

@@ -440,6 +440,7 @@ def tile_equilibrium_mass_balance_s3_kernel(
         lam_mult(0, 0, 1)
         f_scale(0, (1,))
         phi_turn(0, 0, 0)
+        warm_up(128, 4)
         phi_turn(0, 1, 1)
         lam_turn(0, 1, 1, 2)
         warm_up(128, 6)

import math
from contextlib import ExitStack

import concourse.mybir as mybir
from concourse.masks import make_identity

B, E, D, S = 1024, 1024, 512, 2048
FLOPS = 2 * B * S * (E + D) + 2 * B * S * E

F32 = mybir.dt.float32
BF16 = mybir.dt.bfloat16
U32 = mybir.dt.uint32
I32 = mybir.dt.int32
U16 = mybir.dt.uint16
U8 = mybir.dt.uint8
FP8 = mybir.dt.float8_e4m3fn
FP8X4 = mybir.dt.float8_e4m3fn_x4
FP4X4 = mybir.dt.float4_e2m1fn_x4
ALU = mybir.AluOpType
ACT = mybir.ActivationFunctionType

P = 128
HALF = 512
ROWS = 4
UNITS = S // 512
LG = E // 512
FIRST = 2
NB = 3
REGION = {"moving scales": 0, "moving codes": 7168 + 128, "stationary": 7168 + 128 + 20480 + 64}
ADD_ORDER = ((2, 0, 3, 1), (0, 1, 2, 3))
SLOT = {("lam", 0, 0): 0, ("g", 0): 4, ("lam", 1, 0): 0, ("lam", 0, 1): 1, ("g", 1): 5, ("lam", 1, 1): 1,
        ("phi", 0): 2, ("g", 2): 2, ("phi", 1): 3, ("g", 3): 2}
X, Y = (6, 7, 0, 1), (3, 2, 5, 4)
XR = X[2:] + X[:2]
YA, XA = (Y[0], Y[2], Y[1], Y[3]), (XR[0], XR[2], XR[1], XR[3])
ZB = {(0, 0): X, (0, 1): Y, (0, 2): X[:2] + Y[:2], (0, 3): Y[2:] + X[2:], (1, 0): YA, (1, 1): XA, (1, 2): YA, (1, 3): XA}
OB = Y + XR


def tile_equilibrium_mass_balance_s3_kernel(
    tc, lam_bytes, lam_scale, f_words, f_scales, phi, g, m, a_words, a_scales, feed, out
):
    nc = tc.nc
    with ExitStack() as ctx:
        keep = ctx.enter_context(tc.tile_pool(name="keep", bufs=1))
        work = ctx.enter_context(tc.tile_pool(name="work", bufs=2))
        mx = ctx.enter_context(tc.tile_pool(name="mx", bufs=1))
        psum = ctx.enter_context(tc.psum_pool(name="psum", bufs=1))
        ctx.enter_context(tc.manual_schedule())

        lam_v = lam_bytes.rearrange("(h p c) k -> h p c k", h=2, c=ROWS)
        phi_v = phi.rearrange("(h p c) k -> h p c k", h=2, c=ROWS)
        feed_v = feed.rearrange("(h p c) e -> h p c e", h=2, c=ROWS)
        out_v = out.rearrange("(h p c) e -> h p c e", h=2, c=ROWS)
        g_v = g.rearrange("(p j) s -> p j s", j=4)
        a_v = a_words.rearrange("k p b -> p k b")

        cursor = dict(REGION)

        def operand(region, shape, dtype, size, name):
            at = cursor[region]
            cursor[region] = at + size
            return mx.tile(shape, dtype, name=name, offset=at, align_bytes=256 if at == 0 else 64)

        def bank(i):
            return psum.tile([P, 512], F32, name="bank%d" % i)

        def lay(*key):
            return keep.tile([P, 512, 4], BF16, name="lay%d" % SLOT[key], align_bytes=64)

        lam_sb, phi_sb, feed_sb, g_sb, f_sb, f_raw = {}, {}, {}, {}, {}, {}

        def load_lam(h, k):
            lam_sb[h, k] = keep.tile([P, ROWS, 512], U8, name="lam_sb%d%d" % (h, k))
            nc.sync.dma_start(out=lam_sb[h, k][:], in_=lam_v[h][:, :, 512 * k : 512 * (k + 1)])

        def load_lam_rows(pair):
            lam_sb[0, "rows", pair] = keep.tile([P, 2 * E], U8, name="lam_rows%d" % pair)
            nc.sync.dma_start(
                out=lam_sb[0, "rows", pair][:], in_=lam_v[0][:, 2 * pair : 2 * pair + 2].rearrange("p c k -> p (c k)")
            )

        def load_phi(h, pair):
            phi_sb[h, pair] = keep.tile([P, 2 * D], BF16, name="phi_sb%d%d" % (h, pair))
            nc.sync.dma_start(out=phi_sb[h, pair][:], in_=phi_v[h][:, 2 * pair : 2 * pair + 2].rearrange("p c k -> p (c k)"))

        def load_feed(h, pair):
            feed_sb[h, pair] = keep.tile([P, 2, E], BF16, name="g_sb%d" % (2 * h + pair))
            nc.sync.dma_start(out=feed_sb[h, pair][:], in_=feed_v[h][:, 2 * pair : 2 * pair + 2])

        def load_g(u):
            g_sb[u] = keep.tile([P, 4, 512], BF16, name="g_sb%d" % u)
            nc.sync.dma_start(out=g_sb[u][:], in_=g_v[:, :, 512 * u : 512 * (u + 1)])

        def load_f(k, pair):
            f_sb[k, pair] = keep.tile([P, 2048], U8, name="f_sb%d%d" % (k, pair))
            nc.sync.dma_start(out=f_sb[k, pair][:], in_=f_words[k][:, 2048 * pair : 2048 * (pair + 1)])

        def scale_tile(name, passes, width):
            tile = keep.tile([P, passes, width], U8, name=name, align_bytes=64)
            nc.vector.memset(tile[:].bitcast(I32), 0)
            return tile

        def load_scales(dst, src):
            rows = src.bitcast(I32).rearrange("k (q r) n -> r q k n", r=4)
            words = dst[:].bitcast(I32)
            for r in range(4):
                nc.sync.dma_start(out=words[r:P:32], in_=rows[r])

        phi_q, phi_s, lam_q, lam_s, phi_t, lam_t, turned, wide = {}, {}, {}, {}, {}, {}, {}, {}

        def lam_cast(h, k, c, eng):
            if (h, k) not in wide:
                wide[h, k] = work.tile([P, ROWS * 512], BF16, name="wide", tag="wide", bufs=2)
            copy = nc.scalar.copy if eng == "s" else nc.vector.tensor_copy
            copy(wide[h, k][:, 512 * c : 512 * (c + 1)], lam_sb[h, "rows", c // 2][:, E * (c % 2) + 512 * k : E * (c % 2) + 512 * (k + 1)].bitcast(FP8))

        def turn(key, rows, pair, b):
            turned[key] = bank(b)
            words = rows.bitcast(F32)
            for i in range(2):
                c = 2 * pair + i
                for u in range(2):
                    at = 256 * u + 128 * i
                    nc.tensor.transpose(
                        turned[key][:, at : at + 128], words[:, 256 * c + u : 256 * (c + 1) : 2], ident[:]
                    )

        def lam_spread(h, k, first=0, last=2):
            if first == 0:
                wide[h, k] = work.tile([P, ROWS * 512], BF16, name="wide", tag="wide", bufs=2)
            ws = slice(256 * first, 256 * last)
            nc.vector.tensor_scalar(
                out=wide[h, k][:].rearrange("p (u w e) -> p w u e", u=2, e=2)[:, ws],
                in0=lam_sb[h, k][:].rearrange("p c k -> p (c k)").bitcast(FP8).rearrange("p (w u e) -> p w u e", u=2, e=2)[:, ws],
                scalar1=one[:], scalar2=None, op0=ALU.mult,
            )

        def lam_turn_whole(h, k, pair, b):
            turned[h, k, pair] = bank(b)
            words = wide[h, k][:].bitcast(F32)
            for i in range(2):
                for u in range(2):
                    at, src = 256 * u + 128 * i, 512 * u + 128 * (2 * pair + i)
                    nc.tensor.transpose(turned[h, k, pair][:, at : at + 128], words[:, src : src + 128], ident[:])

        def warm_up(cols, b):
            idle = bank(b)
            width = min(cols, P)
            nc.tensor.matmul(
                idle[:, :cols].rearrange("p (b n) -> p b n", n=width), lhsT=ident[:],
                rhs=ident[:, :width].unsqueeze(1).to_broadcast([P, cols // width, width]), start=True, stop=True,
            )

        def lam_turn(h, k, pair, b):
            turn((h, k, pair), wide[h, k][:], pair, b)

        def phi_turn(h, pair, b):
            turn((h, "phi", pair), phi_sb[h, pair][:], 0, b)

        def lam_mult(h, k, pair):
            if pair == 0:
                lam_t[h, k] = lay("lam", h, k)
            nc.vector.tensor_tensor(
                out=lam_t[h, k][:, 256 * pair : 256 * (pair + 1), :].rearrange("p r (u e) -> p r u e", e=2),
                in0=turned[h, k, pair][:].bitcast(BF16).rearrange("p (u r e) -> p r u e", u=2, e=2),
                in1=l_sc[:, k, :].rearrange("p (u e) -> p u e", e=2).unsqueeze(1).to_broadcast([P, 256, 2, 2]),
                op=ALU.mult,
            )

        def phi_copy(h, pair):
            if pair == 0:
                phi_t[h] = lay("phi", h)
            dst = phi_t[h][:].rearrange("p r t -> p (r t)").bitcast(F32).rearrange("p (r u) -> p r u", u=2)
            nc.scalar.copy(
                dst[:, 256 * pair : 256 * (pair + 1)], turned[h, "phi", pair][:].rearrange("p (u r) -> p r u", u=2)
            )

        def quantise(name, src, moving=False):
            codes = operand("moving codes" if moving else "stationary", [P, 512], U32, 2048, name + "_q")
            scales = operand("moving scales" if moving else "stationary", [P, 512], U8, 512, name + "_s")
            nc.vector.quantize_mx(out=codes[:].bitcast(FP8X4), scales=scales[:], in_=src[:].rearrange("p r t -> p (r t)"))
            return codes, scales

        def phi_quant(h):
            phi_q[h], phi_s[h] = quantise("phi%d" % h, phi_t[h], True)

        def lam_quant(h, k):
            lam_q[h, k], lam_s[h, k] = quantise("lam%d%d" % (h, k), lam_t[h, k], True)

        g_q, g_s, f_p, f_sp, g_i = {}, {}, {}, {}, {}

        def g_lay(u, first, last, eng):
            if u not in g_i:
                g_i[u] = lay("g", u)
            ms = slice(8 * first, 8 * last)
            copy = nc.scalar.copy if eng == "s" else nc.vector.tensor_copy
            copy(
                g_i[u][:].rearrange("p (t a b) j -> p a j b t", t=4, b=2)[:, ms],
                g_sb[u][:].rearrange("p j (a b t) -> p a j b t", t=4, b=2)[:, ms],
            )

        def g_lay_pool(u, first, last):
            if u not in g_i:
                g_i[u] = lay("g", u)
            ms = slice(16 * first, 16 * last)
            nc.gpsimd.tensor_scalar(
                out=g_i[u][:].rearrange("p (t m) j -> p t m j", t=4)[:, :, ms],
                in0=g_sb[u][:].rearrange("p j (m t) -> p t m j", t=4)[:, :, ms],
                scalar1=1.0, scalar2=0.0, op0=ALU.mult, op1=ALU.add,
            )

        def g_quant(u):
            g_q[u], g_s[u] = quantise("g%d" % u, g_i[u])

        def f_move(k, first, count=1):
            pair, at = divmod(first, 2)
            if (k, pair) not in f_p:
                f_p[k, pair] = operand("stationary", [P, 2, 1024], U8, 2048, "f_p%d%d" % (k, pair))
            nc.vector.tensor_copy(
                out=f_p[k, pair][:, at : at + count].bitcast(U16).rearrange("p u (t m) -> p u t m", t=4),
                in_=f_sb[k, pair][:].bitcast(U16).rearrange("p (u m t) -> p u t m", u=2, t=4)[:, at : at + count],
            )

        def f_scale(u, ks, eng="v", slot=None):
            if slot is None:
                dst = operand("stationary", [P, len(ks), 512], U8, 512 * len(ks), "f_sp%d%d" % (u, ks[0]))[:]
            else:
                dst = lay(*slot)[:].rearrange("p r t -> p (r t)")[:, : 256 * len(ks)].bitcast(U8).rearrange("p (k n) -> p k n", n=512)
            for i, k in enumerate(ks):
                f_sp[u, k] = dst[:, i, :]
            (nc.gpsimd if eng == "g" else nc.vector).tensor_copy(
                out=dst.rearrange("p k (t m) -> p k t m", t=4),
                in_=f_raw[u // 2][:, ks[0] : ks[-1] + 1, 512 * (u % 2) : 512 * (u % 2 + 1)].rearrange("p k (m t) -> p k t m", t=4),
            )

        e_sb, flat, nb, n_q, n_s, z_ps, pairs = {}, {}, {}, {}, {}, {}, {}

        def z_lam(h, u, t, k, phi_first=False):
            if k == 0 and not phi_first:
                z_ps[h, u, t] = bank(ZB[h, u][t])
            nc.tensor.matmul_mx(
                out=z_ps[h, u, t][:],
                lhsT=f_p[k, u // 2][:, u % 2, 256 * t : 256 * (t + 1)].bitcast(FP4X4),
                lhsT_scale=f_sp[u, k][:, 128 * t : 128 * (t + 1)],
                rhs=lam_q[h, k][:].bitcast(FP8X4),
                rhs_scale=lam_s[h, k][:],
                start=(k == 0 and not phi_first), stop=(k == LG - 1 and phi_first),
            )

        def z_phi(h, u, t, phi_first=False):
            if phi_first:
                z_ps[h, u, t] = bank(ZB[h, u][t])
            cols = slice(128 * t, 128 * (t + 1))
            nc.tensor.matmul_mx(
                out=z_ps[h, u, t][:], lhsT=g_q[u][:, cols].bitcast(FP8X4), lhsT_scale=g_s[u][:, cols],
                rhs=phi_q[h][:].bitcast(FP8X4), rhs_scale=phi_s[h][:], start=phi_first, stop=not phi_first,
            )

        def exp(h, u, t):
            if t == 0:
                e_sb[h, u] = work.tile([P, 4, HALF], F32, name="e_sb", tag="e_sb", bufs=4)
            nc.scalar.activation(e_sb[h, u][:, t, :], z_ps[h, u, t][:], ACT.Exp)

        def exp_pair(h, u, t):
            if t == 0:
                pairs[h, u] = work.tile([P, 2, HALF, 2], BF16, name="pairs", tag="pairs", bufs=4)
            nc.scalar.activation(
                pairs[h, u][:, t // 2, :, t % 2], z_ps[h, u, t][:], ACT.Exp, bias=log_m[:, 4 * u + t : 4 * u + t + 1]
            )

        def n_sign(h, u):
            nb[h, u] = work.tile([P, HALF, 4], BF16, name="nb", tag="nb", bufs=NB, align_bytes=64)
            nc.vector.tensor_tensor(
                out=nb[h, u][:].rearrange("p r (v e) -> p r v e", e=2),
                in0=pairs[h, u][:].rearrange("p v r e -> p r v e"),
                in1=sign_m[:, 4 * u : 4 * u + 4].rearrange("p (v e) -> p v e", e=2).unsqueeze(1).to_broadcast([P, HALF, 2, 2]),
                op=ALU.mult,
            )

        def small(name, dtype=F32):
            return keep.tile([P, UNITS * 4], dtype, name=name)

        def small_stt(name, a, number, op0, b, op1):
            dst = small(name)
            nc.vector.scalar_tensor_tensor(out=dst[:], in0=a[:], scalar=number, in1=b[:], op0=op0, op1=op1)
            return dst

        def small_act(name, src, func, dtype=F32, **kw):
            dst = small(name, dtype)
            nc.scalar.activation(dst[:], src, func, **kw)
            return dst

        def n_scale(h, u, t, cells=HALF):
            if t == 0:
                flat[h, u] = work.tile([P, 4, HALF], BF16, name="flat", tag="wide", bufs=2)
            nc.scalar.activation(
                flat[h, u][:, t, :cells], e_sb[h, u][:, t, :cells], ACT.Copy, scale=m_f[:, 4 * u + t : 4 * u + t + 1]
            )

        def n_lay(h, u, cells=HALF):
            if (h, u) not in nb:
                nb[h, u] = work.tile([P, HALF, 4], BF16, name="nb", tag="nb", bufs=NB, align_bytes=64)
            nc.vector.tensor_copy(
                nb[h, u][:].rearrange("p (r i) t -> p r t i", i=4)[:, : cells // 4],
                flat[h, u][:].rearrange("p t (r i) -> p r t i", i=4)[:, : cells // 4],
            )

        def n_mult(h, u, first=0, last=HALF // 4):
            if (h, u) not in nb:
                nb[h, u] = work.tile([P, HALF, 4], BF16, name="nb", tag="nb", bufs=NB, align_bytes=64)
            nc.vector.tensor_tensor(
                out=nb[h, u][:].rearrange("p (r i) t -> p r t i", i=4)[:, first:last],
                in0=e_sb[h, u][:].rearrange("p t (r i) -> p r t i", i=4)[:, first:last],
                in1=m_f[:, 4 * u : 4 * u + 4].unsqueeze(1).unsqueeze(3).to_broadcast([P, last - first, 4, 4]),
                op=ALU.mult,
            )

        def n_quant(h, u):
            n_q[h, u], n_s[h, u] = quantise("n%d%d" % (h, u), nb[h, u])

        acc = {}

        def balance(h, c, e, first=0, last=UNITS):
            if first == 0:
                acc[h, c, e] = bank(OB[2 * c + e])
            cols = slice(128 * c, 128 * (c + 1))
            for u in ADD_ORDER[h][first:last]:
                nc.tensor.matmul_mx(
                    out=acc[h, c, e][:],
                    lhsT=n_q[h, u][:, cols].bitcast(FP8X4), lhsT_scale=n_s[h, u][:, cols],
                    rhs=a_sb[:, u, 1024 * e : 1024 * (e + 1)].bitcast(FP4X4),
                    rhs_scale=a_sc[:, u, 512 * e : 512 * (e + 1)],
                    start=(u == ADD_ORDER[h][0]), stop=(u == ADD_ORDER[h][-1]),
                )

        def last_columns(h, c, e, banks):
            rows = slice(128 * c, 128 * (c + 1))
            for i, b in enumerate(banks):
                at = 512 * e + 128 * i
                part = bank(b)
                for u in range(UNITS):
                    nc.tensor.matmul_mx(
                        out=part[:, :P],
                        lhsT=n_q[h, u][:, rows].bitcast(FP8X4), lhsT_scale=n_s[h, u][:, rows],
                        rhs=a_sb[:, u, 2 * at : 2 * (at + P)].bitcast(FP4X4), rhs_scale=a_sc[:, u, at : at + P],
                        start=(u == 0), stop=(u == UNITS - 1),
                    )
                o = work.tile([P, P], F32, name="o", tag="o", bufs=10)
                nc.vector.tensor_tensor(out=o[:], in0=part[:, :P], in1=feed_sb[h, c // 2][:, c % 2, at : at + P], op=ALU.subtract)
                (nc.scalar if i % 2 == 0 else nc.sync).dma_start(out=out_v[h][:, c, at : at + P], in_=o[:])

        def finish(h, c, e, parts=1):
            w = 512 // parts
            for i in range(parts):
                cols = slice(512 * e + w * i, 512 * e + w * (i + 1))
                o = work.tile([P, w], F32, name="o", tag="o", bufs=10)
                nc.vector.tensor_tensor(
                    out=o[:], in0=acc[h, c, e][:, w * i : w * (i + 1)], in1=feed_sb[h, c // 2][:, c % 2, cols], op=ALU.subtract
                )
                nc.sync.dma_start(out=out_v[h][:, c, cols], in_=o[:])

        FOUR = range(4)
        APART = (0, 2, 1, 3)

        def z_lams(h, u, k, tiles=FOUR):
            for t in tiles:
                z_lam(h, u, t, k)

        def z_tile(h, u, t):
            for k in range(LG):
                z_lam(h, u, t, k)
            z_phi(h, u, t)
            exp_pair(h, u, t)

        def z_unit(h, u):
            for t in APART:
                z_tile(h, u, t)

        def scale_unit(h, u, cells=HALF):
            for t in FOUR:
                n_scale(h, u, t, cells)


        f_first = scale_tile("f_first", LG, 512 * FIRST)
        ident = keep.tile([P, P], F32, name="ident")
        make_identity(nc, ident[:])
        f_rest = scale_tile("f_rest", LG, S - 512 * FIRST)
        f_raw[0], f_raw[1] = f_first, f_rest
        a_sc = operand("moving scales", [P, UNITS, E], U8, UNITS * E, "a_sc")
        nc.vector.memset(a_sc[:].bitcast(I32), 0)
        l_sc = keep.tile([P, LG, 4], F32, name="l_sc")
        m_sb = keep.tile([P, UNITS, 4], BF16, name="m_sb")
        m_f = keep.tile([P, UNITS * 4], F32, name="m_f")
        a_sb = operand("moving codes", [P, UNITS, 2 * E], U8, UNITS * 2 * E, "a_sb")
        one = keep.tile([P, 1], F32, name="one")
        nc.vector.memset(one[:], 1.0)

        load_lam_rows(0)
        load_f(0, 0)
        load_lam_rows(1)
        nc.sync.dma_start(out=l_sc[:], in_=lam_scale.rearrange("o (k p t) -> p (o k) t", p=P, t=4))
        load_scales(f_first, f_scales[:, :, : 512 * FIRST])
        load_phi(0, 0)
        load_phi(0, 1)
        load_g(0)
        load_phi(1, 0)
        load_phi(1, 1)
        load_f(1, 0)
        load_g(1)
        load_lam(1, 0)
        load_scales(f_rest, f_scales[:, :, 512 * FIRST :])
        load_f(0, 1)
        nc.sync.dma_start(out=m_sb[:], in_=m.rearrange("(u p t) -> p u t", p=P, t=4))
        load_g(2)
        load_f(1, 1)
        load_g(3)
        load_lam(1, 1)
        load_scales(a_sc, a_scales)
        nc.sync.dma_start(out=a_sb[:], in_=a_v)

        warm_up(384, 4)
        lam_cast(0, 0, 0, "v")
        lam_cast(0, 0, 1, "v")
        lam_cast(0, 1, 0, "s")
        lam_cast(0, 1, 1, "s")
        lam_cast(0, 0, 2, "s")
        lam_cast(0, 0, 3, "s")
        lam_turn(0, 0, 0, 6)
        lam_turn(0, 1, 0, 7)
        warm_up(256, 4)
        lam_turn(0, 0, 1, 3)
        f_move(0, 0, 2)
        f_scale(0, (0,), "g")
        f_scale(1, (0,), "g")
        lam_cast(0, 1, 2, "s")
        lam_cast(0, 1, 3, "s")
        lam_mult(0, 0, 0)
        lam_mult(0, 1, 0)
        lam_mult(0, 0, 1)
        f_scale(0, (1,))
        phi_turn(0, 0, 0)
        warm_up(128, 4)
        phi_turn(0, 1, 1)
        lam_turn(0, 1, 1, 2)
        warm_up(128, 6)
        phi_turn(1, 0, 5)
        phi_turn(1, 1, 4)
        lam_quant(0, 0)
        phi_copy(0, 0)
        phi_copy(0, 1)
        g_lay(0, 0, 4, "s")
        phi_copy(1, 0)
        phi_copy(1, 1)
        g_lay(0, 4, 8, "s")
        lam_mult(0, 1, 1)
        z_lams(0, 0, 0)
        z_lams(0, 1, 0)
        f_move(1, 0)
        lam_quant(0, 1)
        phi_quant(0)
        g_quant(0)
        z_lams(0, 0, 1)
        g_lay(1, 0, 6, "s")
        f_move(1, 1)
        f_scale(1, (1,))
        for t in FOUR:
            z_phi(0, 0, t)
            exp(0, 0, t)
        z_lams(0, 1, 1)
        g_lay(1, 6, 8, "v")
        f_move(0, 2, 2)
        g_quant(1)
        for t in FOUR:
            z_phi(0, 1, t)
        m_all = m_sb[:].rearrange("p u t -> p (u t)")
        m_abs = small_act("m_abs", m_all, ACT.Abs)
        sign_m = small_act("sign_m", m_all, ACT.Sign, BF16)
        size = small("size")
        g_lay(2, 0, 4, "s")
        f_scale(2, (0, 1))
        f_move(1, 2, 2)
        lam_spread(1, 0)
        for t in (0, 1):
            for k in range(LG):
                z_lam(0, 2, t, k)
        lam_turn_whole(1, 0, 0, X[2])
        lam_turn_whole(1, 0, 1, X[3])
        g_lay(2, 4, 8, "v")
        f_scale(3, (0, 1))
        nc.vector.tensor_scalar(out=size[:], in0=m_abs[:], scalar1=2.0**-126, scalar2=None, op0=ALU.max)
        for t in (0, 1, 2):
            exp(0, 1, t)
        guess = small_act(
            "guess", size[:].bitcast(U32), ACT.Copy, scale=-math.log(2.0) / 2**23, bias=math.log(2.0) * (127 - 0.043) + 1.5
        )
        exp(0, 1, 3)
        back = small_act("back", guess[:], ACT.Exp, bias=-1.5)
        g_quant(2)
        g_lay_pool(3, 5, 8)
        lam_mult(1, 0, 0)
        lam_mult(1, 0, 1)
        ratio = small("ratio")
        nc.vector.tensor_tensor(out=ratio[:], in0=back[:], in1=size[:], op=ALU.mult)
        for t in (2, 3):
            for k in range(LG):
                z_lam(0, 2, t, k)
        g_lay(3, 0, 4, "s")
        g_lay(3, 4, 5, "v")
        nc.vector.tensor_copy(out=m_f[:], in_=m_sb[:].rearrange("p u t -> p (u t)"))
        z_phi(0, 2, 0)
        exp(0, 2, 0)
        for t in (1, 2, 3):
            z_phi(0, 2, t)
            exp(0, 2, t)
        for i in FOUR:
            load_feed(i // 2, i % 2)
        g_quant(3)
        bend = small_stt("bend", ratio, 4.0, ALU.subtract, ratio, ALU.mult)
        lam_spread(1, 1)
        phi_quant(1)
        lam_quant(1, 0)
        for t in FOUR:
            for k in range(LG):
                z_lam(0, 3, t, k)
        for t in FOUR:
            z_phi(0, 3, t)
        for t in FOUR:
            exp(0, 3, t)
        scale_unit(0, 0)
        lam_turn_whole(1, 1, 0, X[0])
        lam_turn_whole(1, 1, 1, X[1])
        lam_mult(1, 1, 0)
        lam_mult(1, 1, 1)
        closer = small_stt("closer", bend, 0.5, ALU.mult, guess, ALU.add)
        for h, u, t in [(1, u, t) for u in range(2) for t in APART]:
            z_phi(h, u, t, True)
            z_lam(h, u, t, 0, True)
        lam_quant(1, 1)
        n_mult(0, 2, 0, 64)
        n_scale(0, 1, 0)
        back2 = small_act("back2", closer[:], ACT.Exp)
        for t in (1, 2, 3):
            n_scale(0, 1, t)
        ratio2 = small("ratio2")
        nc.vector.tensor_tensor(out=ratio2[:], in0=back2[:], in1=size[:], op=ALU.mult)
        n_mult(0, 2, 64, 128)
        log_m = small_stt("log_m", ratio2, 1.0, ALU.subtract, closer, ALU.subtract)
        n_lay(0, 0)
        n_quant(0, 2)
        for t in APART:
            z_lam(1, 0, t, 1, True)
            exp(1, 0, t)
        for t in APART:
            z_lam(1, 1, t, 1, True)
            exp_pair(1, 1, t)
        n_mult(0, 3)
        n_quant(0, 0)
        n_lay(0, 1)
        n_quant(0, 3)
        n_quant(0, 1)
        n_mult(1, 0)
        z_unit(1, 2)
        z_unit(1, 3)
        n_sign(1, 1)
        n_quant(1, 0)
        for c in FOUR:
            for e in range(2):
                balance(0, c, e)
        n_quant(1, 1)
        finish(0, 0, 0)
        n_sign(1, 2)
        finish(0, 0, 1)
        n_quant(1, 2)
        finish(0, 1, 0)
        n_sign(1, 3)
        finish(0, 1, 1)
        n_quant(1, 3)
        for c in (2, 3):
            for e in range(2):
                finish(0, c, e)
        for e in range(2):
            balance(1, 0, e, 0, UNITS - 1)
        for e in range(2):
            balance(1, 0, e, UNITS - 1)
            finish(1, 0, e)
        for c in (1, 2, 3):
            for e in range(2):
                if (c, e) != (3, 1):
                    balance(1, c, e)
                    finish(1, c, e)
        last_columns(1, 3, 1, (OB[7], OB[0], OB[1], OB[2]))
